import numpy as np
import ml_dtypes


def mxq(x, axis, fmt="e4m3"):
    dtype, down = {"e4m3": (ml_dtypes.float8_e4m3fn, 7), "e5m2": (ml_dtypes.float8_e5m2, 14)}[fmt]
    v = np.moveaxis(np.asarray(x, np.float32).astype(ml_dtypes.bfloat16).astype(np.float64), axis, -1)
    blocks = v.reshape(v.shape[:-1] + (-1, 32))
    amax = np.abs(blocks).max(-1, keepdims=True)
    byte = np.maximum(np.where(amax > 0, np.frexp(amax)[1] - 1 + 127, 0) - down, 1)
    scale = np.exp2(byte - 127.0)
    codes = (blocks / scale).astype(np.float32).astype(dtype).astype(np.float64)
    return np.moveaxis((codes * scale).reshape(v.shape), -1, axis)


WIDE = False


def mx_kscale(k):
    if not WIDE:
        return np.ones(k)
    levels = np.array([10, -10, 5, -5, 0])
    if k % 512:
        return np.exp2(np.random.permutation(np.resize(levels, k // 32))).repeat(32)
    a = np.empty((k // 512, 16))
    for p in range(k // 512):
        a[p, :8] = np.random.permutation(np.resize(levels, 8))
        for g in range(8):
            far = levels[np.abs(levels - a[p, g]) >= 10]
            a[p, g + 8] = far[np.random.randint(len(far))]
    return np.exp2(a.ravel()).repeat(32)


def f64(x):
    return np.asarray(x).astype(np.float64)


def striped(idx):
    return np.tile(idx.reshape(-1, 16).T, (8, 1)).astype(np.uint16)


def unstriped(offs):
    return offs[:16].T.reshape(-1).astype(np.int64)


E2M1 = np.array([0.0, 0.5, 1.0, 1.5, 2.0, 3.0, 4.0, 6.0, -0.0, -0.5, -1.0, -1.5, -2.0, -3.0, -4.0, -6.0])


def pack_weight(w, fmt):
    k, n = w.shape
    w = f64(np.asarray(w, np.float32).astype(ml_dtypes.bfloat16)).reshape(k // 32, 32, n)
    amax = np.abs(w).max(1)
    if fmt == "e4m3":
        byte = np.frexp(amax)[1] - 1 + 127 - 7
    else:
        mant, ex = np.frexp(amax / 6.0)
        byte = np.where(mant > 0.5, ex, ex - 1) + 127
    byte = np.clip(np.where(amax > 0, byte, 1), 1, 254)
    scaled = (w * np.exp2(127.0 - byte)[:, None, :]).reshape(k, n).astype(np.float32)
    by_word = np.ascontiguousarray(scaled.reshape(k // 512, 128, 4, n).transpose(0, 1, 3, 2))
    if fmt == "e4m3":
        words = by_word.astype(ml_dtypes.float8_e4m3fn).view(np.uint8)
    else:
        c = by_word.astype(ml_dtypes.float4_e2m1fn).view(np.uint8) & 0xF
        words = (c[..., 0::2] | (c[..., 1::2] << 4)).reshape(k // 512, 128, 2 * n)
    return np.ascontiguousarray(words), np.ascontiguousarray(byte.astype(np.uint8).reshape(k // 512, 16, n))


def unpack_weight(words, scales, fmt):
    g, _, n = scales.shape
    words = np.ascontiguousarray(words).reshape(g, 128, n, -1)
    if fmt == "e4m3":
        vals = words.view(ml_dtypes.float8_e4m3fn).astype(np.float64)
    else:
        nib = np.empty((g, 128, n, 4), np.uint8)
        nib[..., 0::2] = words & 0xF
        nib[..., 1::2] = words >> 4
        vals = E2M1[nib]
    vals = vals * np.repeat(np.exp2(scales.astype(np.float64) - 127.0), 8, axis=1)[..., None]
    return vals.transpose(0, 1, 3, 2).reshape(g * 512, n)


def silu(v):
    return v / (1.0 + np.exp(-np.maximum(v, -700.0)))


K, T, E, C, F, D, H = 512, 512, 6, 256, 2, 256, 512
N, TOP = 128, 3


def by_expert(wq, xq, E, C):
    return np.concatenate([wq[e].T @ xq[:, e * C:(e + 1) * C] for e in range(E)], axis=1)


def setup_inputs():
    n = np.random.standard_normal
    s = mx_kscale(K)
    u = mx_kscale(H)
    deal = np.repeat(np.arange(E), C).reshape(TOP, T)[:, np.random.permutation(T)]
    deal = np.take_along_axis(deal, np.argsort(np.random.rand(TOP, T), axis=0), axis=0)
    for _ in range(8):
        s_, t_ = np.random.permutation(T).reshape(2, -1); r = np.random.randint(TOP, size=T // 2); x, y = deal[r, s_].copy(), deal[r, t_].copy()
        ok = ~((deal[:, s_] == y).any(0) | (deal[:, t_] == x).any(0)); deal[r[ok], s_[ok]] = y[ok]; deal[r[ok], t_[ok]] = x[ok]
    order = np.lexsort((np.random.rand(TOP * T), deal.reshape(-1)))
    slot_token = order % T; pos = np.empty(TOP * T, np.int64); pos[order] = np.arange(TOP * T); pos = pos.reshape(TOP, T)
    g = np.random.uniform(0.5, 1.5, (TOP, T)); g = g / g.sum(0)
    slots2 = np.random.permutation(T)[:F * D]
    x = pack_weight(n((K, T)) * s[:, None], "e4m3")
    w = [pack_weight(m, "e2m1") for m in n((E, K, N)) / np.sqrt(K) / s[None, :, None]]
    wa = [pack_weight(m, "e2m1") for m in n((F, K, H)) / np.sqrt(K) / s[None, :, None] * u]
    wb = [pack_weight(m, "e2m1") for m in n((F, H, N)) / np.sqrt(H) / u[None, :, None]]
    return {
        "x_words": x[0],
        "x_scales": x[1],
        "w_words": np.stack([m[0] for m in w]),
        "w_scales": np.stack([m[1] for m in w]),
        "wa_words": np.stack([m[0] for m in wa]),
        "wa_scales": np.stack([m[1] for m in wa]),
        "wb_words": np.stack([m[0] for m in wb]),
        "wb_scales": np.stack([m[1] for m in wb]),
        "gate": np.stack([np.tile(r, (128, 1)) for r in g]).astype(np.float32),
        "gate2": (np.tile(np.random.uniform(0.2, 1.0, F * D), (128, 1))).astype(np.float32),
        "offs": striped(slot_token),
        "pos1": striped(pos[0]),
        "pos2": striped(pos[1]),
        "pos3": striped(pos[2]),
        "offs2": striped(slots2),
    }


def reference(x_words, x_scales, w_words, w_scales, wa_words, wa_scales, wb_words, wb_scales, gate, gate2, offs, pos1, pos2, pos3, offs2):
    w = np.stack([unpack_weight(w_words[e], w_scales[e], "e2m1") for e in range(E)])
    wa = np.stack([unpack_weight(wa_words[e], wa_scales[e], "e2m1") for e in range(F)])
    wb = np.stack([unpack_weight(wb_words[e], wb_scales[e], "e2m1") for e in range(F)])
    idx, idx2 = unstriped(offs), unstriped(offs2)
    x = unpack_weight(x_words, x_scales, "e4m3")
    y = by_expert(w, x[:, idx], E, C)
    h = silu(by_expert(wa, x[:, idx2], F, D))
    z = by_expert(wb, mxq(h, 0, "e4m3"), F, D)
    out = sum(f64(gate[r, :1]) * y[:, unstriped(p)] for r, p in enumerate((pos1, pos2, pos3)))
    out[:, idx2] += f64(gate2[:1]) * z
    return out

@@ -1,0 +1,186 @@
+from contextlib import ExitStack
+
+import concourse.mybir as mybir
+from concourse.masks import make_identity
+
+K, T, E, C, F, D, H, N, TOP = 512, 512, 6, 256, 2, 256, 512, 128, 3
+S = E * C
+A = F * D
+P = 128
+WINDOW = 1024
+FLOPS = 2 * K * N * S + 2 * K * H * A + 2 * H * N * A
+
+F32 = mybir.dt.float32
+BF16 = mybir.dt.bfloat16
+I32 = mybir.dt.int32
+U32 = mybir.dt.uint32
+U16 = mybir.dt.uint16
+U8 = mybir.dt.uint8
+FP8X4 = mybir.dt.float8_e4m3fn_x4
+FP4X4 = mybir.dt.float4_e2m1fn_x4
+MULT = mybir.AluOpType.mult
+ADD = mybir.AluOpType.add
+SILU = mybir.ActivationFunctionType.Silu
+
+
+def tile_moe_mlr_silu_kernel(
+    tc, x_words, x_scales, w_words, w_scales, wa_words, wa_scales, wb_words, wb_scales,
+    gate, gate2, offs, pos1, pos2, pos3, offs2, out,
+):
+    nc = tc.nc
+    with ExitStack() as ctx:
+        keep = ctx.enter_context(tc.tile_pool(name="keep", bufs=1))
+        stage = ctx.enter_context(tc.tile_pool(name="stage", bufs=2))
+        ps_h = ctx.enter_context(tc.psum_pool(name="ps_h", bufs=2))
+        ps_t = ctx.enter_context(tc.psum_pool(name="ps_t", bufs=2))
+        ps_y = ctx.enter_context(tc.psum_pool(name="ps_y", bufs=3))
+        ps_z = ctx.enter_context(tc.psum_pool(name="ps_z", bufs=1))
+
+        def load_list(name, src):
+            t = keep.tile([P, src.shape[1]], U16, name=name)
+            nc.sync.dma_start(t[:], src)
+            return t
+
+        def load_words(name, src):
+            count, width = src.shape[0], src.shape[3]
+            t = keep.tile([P, count * width], U8, name=name, align_bytes=64)
+            nc.sync.dma_start(
+                t[:].bitcast(I32).rearrange("p (e w) -> p e w", e=count),
+                src[:, 0].bitcast(I32).rearrange("e p w -> p e w"),
+            )
+            return t
+
+        def load_plane(plane, src):
+            count, width = src.shape[0], src.shape[2]
+            for r in range(4):
+                nc.sync.dma_start(
+                    plane[r:P:32, 0 : count * width].bitcast(I32).rearrange("q (e w) -> q e w", e=count),
+                    src[:, r:16:4, :].bitcast(I32).rearrange("e q w -> q e w"),
+                )
+
+        def zeroed_plane(name, width):
+            t = keep.tile([P, width], U8, name=name, align_bytes=64)
+            nc.vector.memset(t[:].bitcast(I32), 0)
+            return t
+
+        tok_words = keep.tile([P, WINDOW], I32, name="tok_words", align_bytes=64)
+        nc.scalar.dma_start(tok_words[:, 0:T], x_words[0].rearrange("p t d -> p (t d)").bitcast(I32))
+        tok_scales = zeroed_plane("tok_scales", WINDOW)
+        nc.vector.memset(tok_words[:, T:WINDOW], 0)
+        wa_plane = zeroed_plane("wa_plane", F * H)
+        w_plane = zeroed_plane("w_plane", E * N)
+        wb_plane = zeroed_plane("wb_plane", F * N)
+
+        warm = keep.tile([P, 8], F32, name="warm")
+        nc.gpsimd.memset(warm[:], 0.0)
+        nc.scalar.activation(warm[:, 4:5], warm[:, 0:1], SILU)
+        ident = keep.tile([P, P], BF16, name="ident")
+        make_identity(nc, ident[:])
+
+        offs2_sb = load_list("offs2_sb", offs2)
+        offs_sb = load_list("offs_sb", offs)
+        load_plane(tok_scales, x_scales)
+        wa_sb = load_words("wa_sb", wa_words)
+        load_plane(wa_plane, wa_scales[:, 0])
+        w_sb = load_words("w_sb", w_words)
+        load_plane(w_plane, w_scales[:, 0])
+        wb_sb = load_words("wb_sb", wb_words)
+        load_plane(wb_plane, wb_scales[:, 0])
+        gate2_sb = keep.tile([P, A], F32, name="gate2_sb")
+        nc.sync.dma_start(gate2_sb[:], gate2)
+        pos_sb = [load_list("pos1_sb", pos1), load_list("pos2_sb", pos2), load_list("pos3_sb", pos3)]
+        gate_sb = keep.tile([P, TOP, T], F32, name="gate_sb")
+        nc.sync.dma_start(gate_sb[:], gate.rearrange("r p t -> p r t"))
+
+        word_window = tok_words[:].bitcast(U32)
+
+        a_words = keep.tile([P, A], U32, name="a_words", align_bytes=64)
+        a_scales = keep.tile([P, A], U8, name="a_scales", align_bytes=64)
+        nc.vector.tensor_copy(a_words[:], word_window.indirect(offs2_sb[:]))
+        nc.vector.tensor_copy(a_scales[:], tok_scales[:].indirect(offs2_sb[:]))
+
+        h_grouped = keep.tile([P, A, 4], BF16, name="h_grouped", align_bytes=64)
+        for b in range(A // P):
+            f = b * P // D
+            slots = slice(b * P, (b + 1) * P)
+            pre = ps_h.tile([P, H], F32, name="pre")
+            nc.tensor.matmul_mx(
+                out=pre[:],
+                lhsT=a_words[:, slots].bitcast(FP8X4), lhsT_scale=a_scales[:, slots],
+                rhs=wa_sb[:, 2 * f * H : 2 * (f + 1) * H].bitcast(FP4X4), rhs_scale=wa_plane[:, f * H : (f + 1) * H],
+                start=True, stop=True,
+            )
+            act = stage.tile([P, 4, P], BF16, name="act")
+            nc.scalar.activation(act[:], pre[:].rearrange("m (q t) -> m t q", t=4), SILU)
+            turned = ps_t.tile([P, 4, P], BF16, name="turned")
+            for t in range(4):
+                nc.tensor.transpose(turned[:, t, :], act[:, t, :], ident[:])
+            nc.scalar.copy(h_grouped[:, slots, :], turned[:].rearrange("q t m -> q m t"))
+
+        e_words = keep.tile([P, S], U32, name="e_words", align_bytes=64)
+        e_scales = keep.tile([P, S], U8, name="e_scales", align_bytes=64)
+        y_sb = keep.tile([P, S], F32, name="y_sb")
+        half = S // 2
+
+        def gather_half(dst, window, u):
+            nc.vector.tensor_copy(
+                dst[:, u * half : (u + 1) * half], window.indirect(offs_sb[:, u * half // 16 : (u + 1) * half // 16])
+            )
+
+        def experts(first, count):
+            bank = ps_y.tile([P, 2 * C], F32, name="bank")
+            for j in range(count):
+                e = first + j
+                slots = slice(e * C, (e + 1) * C)
+                nc.tensor.matmul_mx(
+                    out=bank[:, j * C : (j + 1) * C],
+                    lhsT=w_sb[:, 2 * e * N : 2 * (e + 1) * N].bitcast(FP4X4), lhsT_scale=w_plane[:, e * N : (e + 1) * N],
+                    rhs=e_words[:, slots].bitcast(FP8X4), rhs_scale=e_scales[:, slots],
+                    start=True, stop=True,
+                )
+            nc.scalar.copy(y_sb[:, first * C : (first + count) * C], bank[:, 0 : count * C])
+
+        gather_half(e_words, word_window, 0)
+        gather_half(e_words, word_window, 1)
+        gather_half(e_scales, tok_scales[:], 0)
+        experts(0, 2)
+        experts(2, 1)
+
+        h_codes = keep.tile([P, A], U32, name="h_codes", align_bytes=64)
+        h_plane = keep.tile([P, A], U8, name="h_plane", align_bytes=64)
+        nc.vector.quantize_mx(
+            out=h_codes[:].bitcast(FP8X4), scales=h_plane[:], in_=h_grouped[:].rearrange("q m t -> q (m t)")
+        )
+        z_bank = ps_z.tile([P, A], F32, name="z_bank")
+        for f in range(F):
+            slots = slice(f * D, (f + 1) * D)
+            nc.tensor.matmul_mx(
+                out=z_bank[:, slots],
+                lhsT=wb_sb[:, 2 * f * N : 2 * (f + 1) * N].bitcast(FP4X4), lhsT_scale=wb_plane[:, f * N : (f + 1) * N],
+                rhs=h_codes[:, slots].bitcast(FP8X4), rhs_scale=h_plane[:, slots],
+                start=True, stop=True,
+            )
+        z_sb = keep.tile([P, A], F32, name="z_sb")
+        nc.scalar.copy(z_sb[:], z_bank[:])
+
+        gather_half(e_scales, tok_scales[:], 1)
+        experts(3, 2)
+        experts(5, 1)
+
+        placed = keep.tile([P, WINDOW], F32, name="placed")
+        nc.vector.tensor_tensor(placed[:].indirect(offs2_sb[:]), z_sb[:], gate2_sb[:], MULT)
+
+        terms = keep.tile([P, TOP, T], F32, name="terms")
+        part = keep.tile([P, 2, T], F32, name="part")
+        res = keep.tile([P, T], F32, name="res")
+        hT = T // 2
+        nc.vector.tensor_tensor(terms[:, 0, :], y_sb[:].indirect(pos_sb[0][:]), gate_sb[:, 0, :], MULT)
+        nc.vector.tensor_tensor(terms[:, 1, :], y_sb[:].indirect(pos_sb[1][:]), gate_sb[:, 1, :], MULT)
+        nc.vector.tensor_tensor(part[:, 0, :], terms[:, 0, :], placed[:, 0:T], ADD)
+        nc.vector.tensor_tensor(terms[:, 2, 0:hT], y_sb[:].indirect(pos_sb[2][:, 0 : hT // 16]), gate_sb[:, 2, 0:hT], MULT)
+        nc.vector.tensor_tensor(part[:, 1, :], part[:, 0, :], terms[:, 1, :], ADD)
+        nc.vector.tensor_tensor(terms[:, 2, hT:T], y_sb[:].indirect(pos_sb[2][:, hT // 16 : T // 16]), gate_sb[:, 2, hT:T], MULT)
+        for u in range(2):
+            cols = slice(u * hT, (u + 1) * hT)
+            nc.vector.tensor_tensor(res[:, cols], part[:, 1, cols], terms[:, 2, cols], ADD)
+            nc.sync.dma_start(out[:, cols], res[:, cols])

@@ -20,6 +20,7 @@ FP8X4 = mybir.dt.float8_e4m3fn_x4
 FP4X4 = mybir.dt.float4_e2m1fn_x4
 MULT = mybir.AluOpType.mult
 ADD = mybir.AluOpType.add
+COPY = mybir.ActivationFunctionType.Copy
 SILU = mybir.ActivationFunctionType.Silu
 
 
@@ -41,10 +42,10 @@ def tile_moe_mlr_silu_kernel(
             nc.sync.dma_start(t[:], src)
             return t
 
-        def load_words(name, src):
+        def load_words(name, src, queue):
             count, width = src.shape[0], src.shape[3]
             t = keep.tile([P, count * width], U8, name=name, align_bytes=64)
-            nc.sync.dma_start(
+            queue.dma_start(
                 t[:].bitcast(I32).rearrange("p (e w) -> p e w", e=count),
                 src[:, 0].bitcast(I32).rearrange("e p w -> p e w"),
             )
@@ -64,33 +65,36 @@ def tile_moe_mlr_silu_kernel(
             return t
 
         tok_words = keep.tile([P, WINDOW], I32, name="tok_words", align_bytes=64)
-        nc.scalar.dma_start(tok_words[:, 0:T], x_words[0].rearrange("p t d -> p (t d)").bitcast(I32))
+        nc.sync.dma_start(tok_words[:, 0:T], x_words[0].rearrange("p t d -> p (t d)").bitcast(I32))
         tok_scales = zeroed_plane("tok_scales", WINDOW)
-        nc.vector.memset(tok_words[:, T:WINDOW], 0)
         wa_plane = zeroed_plane("wa_plane", F * H)
         w_plane = zeroed_plane("w_plane", E * N)
         wb_plane = zeroed_plane("wb_plane", F * N)
+        nc.vector.memset(tok_words[:, T:WINDOW], 0)
 
         warm = keep.tile([P, 8], F32, name="warm")
         nc.gpsimd.memset(warm[:], 0.0)
         nc.scalar.activation(warm[:, 4:5], warm[:, 0:1], SILU)
         ident = keep.tile([P, P], BF16, name="ident")
         make_identity(nc, ident[:])
+        ident32 = keep.tile([P, P], F32, name="ident32")
+        make_identity(nc, ident32[:])
 
         offs2_sb = load_list("offs2_sb", offs2)
-        offs_sb = load_list("offs_sb", offs)
         load_plane(tok_scales, x_scales)
-        wa_sb = load_words("wa_sb", wa_words)
+        wa_sb = load_words("wa_sb", wa_words, nc.sync)
+        offs_sb = load_list("offs_sb", offs)
         load_plane(wa_plane, wa_scales[:, 0])
-        w_sb = load_words("w_sb", w_words)
+        w_sb = load_words("w_sb", w_words, nc.gpsimd)
         load_plane(w_plane, w_scales[:, 0])
-        wb_sb = load_words("wb_sb", wb_words)
+        wb_sb = load_words("wb_sb", wb_words, nc.gpsimd)
         load_plane(wb_plane, wb_scales[:, 0])
-        gate2_sb = keep.tile([P, A], F32, name="gate2_sb")
-        nc.sync.dma_start(gate2_sb[:], gate2)
+        slot_gate = keep.tile([P, A // P], F32, name="slot_gate")
+        with nc.allow_non_contiguous_dma(reason="one weight a partition"):
+            nc.gpsimd.dma_start(slot_gate[:], gate2[0].rearrange("(b m) -> m b", m=P))
         pos_sb = [load_list("pos1_sb", pos1), load_list("pos2_sb", pos2), load_list("pos3_sb", pos3)]
         gate_sb = keep.tile([P, TOP, T], F32, name="gate_sb")
-        nc.sync.dma_start(gate_sb[:], gate.rearrange("r p t -> p r t"))
+        nc.gpsimd.dma_start(gate_sb[:], gate.rearrange("r p t -> p r t"))
 
         word_window = tok_words[:].bitcast(U32)
 
@@ -120,12 +124,10 @@ def tile_moe_mlr_silu_kernel(
         e_words = keep.tile([P, S], U32, name="e_words", align_bytes=64)
         e_scales = keep.tile([P, S], U8, name="e_scales", align_bytes=64)
         y_sb = keep.tile([P, S], F32, name="y_sb")
-        half = S // 2
 
-        def gather_half(dst, window, u):
-            nc.vector.tensor_copy(
-                dst[:, u * half : (u + 1) * half], window.indirect(offs_sb[:, u * half // 16 : (u + 1) * half // 16])
-            )
+        def gather_experts(dst, window, first, count):
+            lo, hi = first * C, (first + count) * C
+            nc.vector.tensor_copy(dst[:, lo:hi], window.indirect(offs_sb[:, lo // 16 : hi // 16]))
 
         def experts(first, count):
             bank = ps_y.tile([P, 2 * C], F32, name="bank")
@@ -140,47 +142,73 @@ def tile_moe_mlr_silu_kernel(
                 )
             nc.scalar.copy(y_sb[:, first * C : (first + count) * C], bank[:, 0 : count * C])
 
-        gather_half(e_words, word_window, 0)
-        gather_half(e_words, word_window, 1)
-        gather_half(e_scales, tok_scales[:], 0)
+        gather_experts(e_words, word_window, 0, 3)
+        gather_experts(e_words, word_window, 3, 3)
+        gather_experts(e_scales, tok_scales[:], 0, 3)
         experts(0, 2)
         experts(2, 1)
+        gather_experts(e_scales, tok_scales[:], 3, 2)
+        experts(3, 2)
+        gather_experts(e_scales, tok_scales[:], 5, 1)
+        experts(5, 1)
 
         h_codes = keep.tile([P, A], U32, name="h_codes", align_bytes=64)
         h_plane = keep.tile([P, A], U8, name="h_plane", align_bytes=64)
         nc.vector.quantize_mx(
             out=h_codes[:].bitcast(FP8X4), scales=h_plane[:], in_=h_grouped[:].rearrange("q m t -> q (m t)")
         )
-        z_bank = ps_z.tile([P, A], F32, name="z_bank")
-        for f in range(F):
-            slots = slice(f * D, (f + 1) * D)
+        z_bank = ps_z.tile([P, A // P, N], F32, name="z_bank")
+        z_gated = keep.tile([P, A // P, N], F32, name="z_gated")
+        for b in range(A // P):
+            f = b * P // D
+            slots = slice(b * P, (b + 1) * P)
             nc.tensor.matmul_mx(
-                out=z_bank[:, slots],
-                lhsT=wb_sb[:, 2 * f * N : 2 * (f + 1) * N].bitcast(FP4X4), lhsT_scale=wb_plane[:, f * N : (f + 1) * N],
-                rhs=h_codes[:, slots].bitcast(FP8X4), rhs_scale=h_plane[:, slots],
+                out=z_bank[:, b, :],
+                lhsT=h_codes[:, slots].bitcast(FP8X4), lhsT_scale=h_plane[:, slots],
+                rhs=wb_sb[:, 2 * f * N : 2 * (f + 1) * N].bitcast(FP4X4), rhs_scale=wb_plane[:, f * N : (f + 1) * N],
                 start=True, stop=True,
             )
+        for b in range(A // P):
+            nc.scalar.activation(z_gated[:, b, :], z_bank[:, b, :], COPY, scale=slot_gate[:, b : b + 1])
+        z_back = ps_h.tile([P, H], F32, name="pre")
+        for b in range(A // P):
+            nc.tensor.transpose(z_back[:, b * P : (b + 1) * P], z_gated[:, b, :], ident32[:])
         z_sb = keep.tile([P, A], F32, name="z_sb")
-        nc.scalar.copy(z_sb[:], z_bank[:])
-
-        gather_half(e_scales, tok_scales[:], 1)
-        experts(3, 2)
-        experts(5, 1)
-
-        placed = keep.tile([P, WINDOW], F32, name="placed")
-        nc.vector.tensor_tensor(placed[:].indirect(offs2_sb[:]), z_sb[:], gate2_sb[:], MULT)
+        nc.scalar.copy(z_sb[:], z_back[:])
 
         terms = keep.tile([P, TOP, T], F32, name="terms")
-        part = keep.tile([P, 2, T], F32, name="part")
-        res = keep.tile([P, T], F32, name="res")
         hT = T // 2
-        nc.vector.tensor_tensor(terms[:, 0, :], y_sb[:].indirect(pos_sb[0][:]), gate_sb[:, 0, :], MULT)
-        nc.vector.tensor_tensor(terms[:, 1, :], y_sb[:].indirect(pos_sb[1][:]), gate_sb[:, 1, :], MULT)
-        nc.vector.tensor_tensor(part[:, 0, :], terms[:, 0, :], placed[:, 0:T], ADD)
-        nc.vector.tensor_tensor(terms[:, 2, 0:hT], y_sb[:].indirect(pos_sb[2][:, 0 : hT // 16]), gate_sb[:, 2, 0:hT], MULT)
-        nc.vector.tensor_tensor(part[:, 1, :], part[:, 0, :], terms[:, 1, :], ADD)
-        nc.vector.tensor_tensor(terms[:, 2, hT:T], y_sb[:].indirect(pos_sb[2][:, hT // 16 : T // 16]), gate_sb[:, 2, hT:T], MULT)
+        sums = [ps_t.tile([P, P], F32, name="turned") for b in range(2)] + [ps_y.tile([P, P], F32, name="bank") for b in range(2)]
+        sums_sb = keep.tile([P, T // P, N], F32, name="sums_sb")
+        back = ps_h.tile([P, T], F32, name="pre")
+
+        def term(r, lo, hi):
+            nc.vector.tensor_tensor(
+                terms[:, r, lo:hi], y_sb[:].indirect(pos_sb[r][:, lo // 16 : hi // 16]), gate_sb[:, r, lo:hi], MULT
+            )
+            for b in range(lo // P, hi // P):
+                nc.tensor.matmul(
+                    sums[b][:], terms[:, r, b * P : (b + 1) * P], ident32[:],
+                    start=(r == 0), stop=(r == TOP - 1), is_transpose=True,
+                )
+
+        def turn_back(lo, hi):
+            for b in range(lo // P, hi // P):
+                nc.scalar.copy(sums_sb[:, b, :], sums[b][:])
+            for b in range(lo // P, hi // P):
+                nc.tensor.transpose(back[:, b * P : (b + 1) * P], sums_sb[:, b, :], ident32[:])
+
+        term(0, 0, T)
+        term(1, 0, T)
+        term(2, 0, hT)
+        turn_back(0, hT)
+        term(2, hT, T)
+        turn_back(hT, T)
+
+        placed = keep.tile([P, WINDOW], F32, name="placed")
+        nc.vector.tensor_copy(placed[:].indirect(offs2_sb[:]), z_sb[:])
+        res = keep.tile([P, T], F32, name="res")
         for u in range(2):
             cols = slice(u * hT, (u + 1) * hT)
-            nc.vector.tensor_tensor(res[:, cols], part[:, 1, cols], terms[:, 2, cols], ADD)
+            nc.vector.tensor_tensor(res[:, cols], back[:, cols], placed[:, cols], ADD)
             nc.sync.dma_start(out[:, cols], res[:, cols])

@@ -34,7 +34,7 @@ def tile_moe_mlr_silu_kernel(
         stage = ctx.enter_context(tc.tile_pool(name="stage", bufs=2))
         ps_h = ctx.enter_context(tc.psum_pool(name="ps_h", bufs=2))
         ps_t = ctx.enter_context(tc.psum_pool(name="ps_t", bufs=2))
-        ps_y = ctx.enter_context(tc.psum_pool(name="ps_y", bufs=3))
+        ps_y = ctx.enter_context(tc.psum_pool(name="ps_y", bufs=2))
         ps_z = ctx.enter_context(tc.psum_pool(name="ps_z", bufs=1))
 
         def load_list(name, src):
@@ -75,8 +75,6 @@ def tile_moe_mlr_silu_kernel(
         warm = keep.tile([P, 8], F32, name="warm")
         nc.gpsimd.memset(warm[:], 0.0)
         nc.scalar.activation(warm[:, 4:5], warm[:, 0:1], SILU)
-        ident = keep.tile([P, P], BF16, name="ident")
-        make_identity(nc, ident[:])
         ident32 = keep.tile([P, P], F32, name="ident32")
         make_identity(nc, ident32[:])
 
@@ -86,15 +84,15 @@ def tile_moe_mlr_silu_kernel(
         offs_sb = load_list("offs_sb", offs)
         load_plane(wa_plane, wa_scales[:, 0])
         w_sb = load_words("w_sb", w_words, nc.gpsimd)
+        gate_sb = keep.tile([P, TOP, T], F32, name="gate_sb")
+        nc.gpsimd.dma_start(gate_sb[:], gate.rearrange("r p t -> p r t"))
         load_plane(w_plane, w_scales[:, 0])
-        wb_sb = load_words("wb_sb", wb_words, nc.gpsimd)
+        wb_sb = load_words("wb_sb", wb_words, nc.sync)
         load_plane(wb_plane, wb_scales[:, 0])
         slot_gate = keep.tile([P, A // P], F32, name="slot_gate")
         with nc.allow_non_contiguous_dma(reason="one weight a partition"):
-            nc.gpsimd.dma_start(slot_gate[:], gate2[0].rearrange("(b m) -> m b", m=P))
+            nc.sync.dma_start(slot_gate[:], gate2[0].rearrange("(b m) -> m b", m=P))
         pos_sb = [load_list("pos1_sb", pos1), load_list("pos2_sb", pos2), load_list("pos3_sb", pos3)]
-        gate_sb = keep.tile([P, TOP, T], F32, name="gate_sb")
-        nc.gpsimd.dma_start(gate_sb[:], gate.rearrange("r p t -> p r t"))
 
         word_window = tok_words[:].bitcast(U32)
 
@@ -114,12 +112,16 @@ def tile_moe_mlr_silu_kernel(
                 rhs=wa_sb[:, 2 * f * H : 2 * (f + 1) * H].bitcast(FP4X4), rhs_scale=wa_plane[:, f * H : (f + 1) * H],
                 start=True, stop=True,
             )
-            act = stage.tile([P, 4, P], BF16, name="act")
-            nc.scalar.activation(act[:], pre[:].rearrange("m (q t) -> m t q", t=4), SILU)
-            turned = ps_t.tile([P, 4, P], BF16, name="turned")
-            for t in range(4):
-                nc.tensor.transpose(turned[:, t, :], act[:, t, :], ident[:])
-            nc.scalar.copy(h_grouped[:, slots, :], turned[:].rearrange("q t m -> q m t"))
+            act = stage.tile([P, 2, P, 2], BF16, name="act")
+            nc.scalar.activation(act[:], pre[:].rearrange("m (q u v) -> m u q v", u=2, v=2), SILU)
+            pairs = act[:].rearrange("m u q v -> m (u q v)").bitcast(F32)
+            turned = ps_t.tile([P, 2, P], F32, name="turned")
+            for u in range(2):
+                nc.tensor.transpose(turned[:, u, :], pairs[:, u * P : (u + 1) * P], ident32[:])
+            nc.scalar.copy(
+                h_grouped[:, slots, :].rearrange("q m t -> q (m t)").bitcast(F32).rearrange("q (m u) -> q m u", u=2),
+                turned[:].rearrange("q u m -> q m u"),
+            )
 
         e_words = keep.tile([P, S], U32, name="e_words", align_bytes=64)
         e_scales = keep.tile([P, S], U8, name="e_scales", align_bytes=64)
@@ -130,7 +132,7 @@ def tile_moe_mlr_silu_kernel(
             nc.vector.tensor_copy(dst[:, lo:hi], window.indirect(offs_sb[:, lo // 16 : hi // 16]))
 
         def experts(first, count):
-            bank = ps_y.tile([P, 2 * C], F32, name="bank")
+            bank = ps_t.tile([P, 2 * C], F32, name="turned")
             for j in range(count):
                 e = first + j
                 slots = slice(e * C, (e + 1) * C)
@@ -208,7 +210,6 @@ def tile_moe_mlr_silu_kernel(
         placed = keep.tile([P, WINDOW], F32, name="placed")
         nc.vector.tensor_copy(placed[:].indirect(offs2_sb[:]), z_sb[:])
         res = keep.tile([P, T], F32, name="res")
-        for u in range(2):
-            cols = slice(u * hT, (u + 1) * hT)
+        for cols in (slice(0, T - P), slice(T - P, T)):
             nc.vector.tensor_tensor(res[:, cols], back[:, cols], placed[:, cols], ADD)
             nc.sync.dma_start(out[:, cols], res[:, cols])

@@ -33,7 +33,7 @@ def tile_moe_mlr_silu_kernel(
         keep = ctx.enter_context(tc.tile_pool(name="keep", bufs=1))
         stage = ctx.enter_context(tc.tile_pool(name="stage", bufs=2))
         ps_h = ctx.enter_context(tc.psum_pool(name="ps_h", bufs=2))
-        ps_t = ctx.enter_context(tc.psum_pool(name="ps_t", bufs=2))
+        ps_t = ctx.enter_context(tc.psum_pool(name="ps_t", bufs=3))
         ps_y = ctx.enter_context(tc.psum_pool(name="ps_y", bufs=2))
         ps_z = ctx.enter_context(tc.psum_pool(name="ps_z", bufs=1))
 
@@ -84,10 +84,10 @@ def tile_moe_mlr_silu_kernel(
         offs_sb = load_list("offs_sb", offs)
         load_plane(wa_plane, wa_scales[:, 0])
         w_sb = load_words("w_sb", w_words, nc.gpsimd)
-        gate_sb = keep.tile([P, TOP, T], F32, name="gate_sb")
-        nc.gpsimd.dma_start(gate_sb[:], gate.rearrange("r p t -> p r t"))
+        wb_sb = load_words("wb_sb", wb_words, nc.gpsimd)
         load_plane(w_plane, w_scales[:, 0])
-        wb_sb = load_words("wb_sb", wb_words, nc.sync)
+        gate_sb = keep.tile([P, TOP, T], F32, name="gate_sb")
+        nc.sync.dma_start(gate_sb[:], gate.rearrange("r p t -> p r t"))
         load_plane(wb_plane, wb_scales[:, 0])
         slot_gate = keep.tile([P, A // P], F32, name="slot_gate")
         with nc.allow_non_contiguous_dma(reason="one weight a partition"):
@@ -127,32 +127,32 @@ def tile_moe_mlr_silu_kernel(
         e_scales = keep.tile([P, S], U8, name="e_scales", align_bytes=64)
         y_sb = keep.tile([P, S], F32, name="y_sb")
 
-        def gather_experts(dst, window, first, count):
-            lo, hi = first * C, (first + count) * C
+        def gather_slots(dst, window, lo, hi):
             nc.vector.tensor_copy(dst[:, lo:hi], window.indirect(offs_sb[:, lo // 16 : hi // 16]))
 
-        def experts(first, count):
+        def experts(lo, hi):
             bank = ps_t.tile([P, 2 * C], F32, name="turned")
-            for j in range(count):
-                e = first + j
-                slots = slice(e * C, (e + 1) * C)
+            for e in range(lo // C, (hi - 1) // C + 1):
+                slots = slice(max(lo, e * C), min(hi, (e + 1) * C))
                 nc.tensor.matmul_mx(
-                    out=bank[:, j * C : (j + 1) * C],
+                    out=bank[:, slots.start - lo : slots.stop - lo],
                     lhsT=w_sb[:, 2 * e * N : 2 * (e + 1) * N].bitcast(FP4X4), lhsT_scale=w_plane[:, e * N : (e + 1) * N],
                     rhs=e_words[:, slots].bitcast(FP8X4), rhs_scale=e_scales[:, slots],
                     start=True, stop=True,
                 )
-            nc.scalar.copy(y_sb[:, first * C : (first + count) * C], bank[:, 0 : count * C])
+            nc.scalar.copy(y_sb[:, lo:hi], bank[:, 0 : hi - lo])
 
-        gather_experts(e_words, word_window, 0, 3)
-        gather_experts(e_words, word_window, 3, 3)
-        gather_experts(e_scales, tok_scales[:], 0, 3)
-        experts(0, 2)
-        experts(2, 1)
-        gather_experts(e_scales, tok_scales[:], 3, 2)
-        experts(3, 2)
-        gather_experts(e_scales, tok_scales[:], 5, 1)
-        experts(5, 1)
+        gather_slots(e_words, word_window, 0, 768)
+        gather_slots(e_words, word_window, 768, S)
+        gather_slots(e_scales, tok_scales[:], 0, 768)
+        experts(0, 512)
+        experts(512, 768)
+        gather_slots(e_scales, tok_scales[:], 768, 1152)
+        experts(768, 1152)
+        gather_slots(e_scales, tok_scales[:], 1152, 1408)
+        experts(1152, 1408)
+        gather_slots(e_scales, tok_scales[:], 1408, S)
+        experts(1408, S)
 
         h_codes = keep.tile([P, A], U32, name="h_codes", align_bytes=64)
         h_plane = keep.tile([P, A], U8, name="h_plane", align_bytes=64)
@@ -210,6 +210,6 @@ def tile_moe_mlr_silu_kernel(
         placed = keep.tile([P, WINDOW], F32, name="placed")
         nc.vector.tensor_copy(placed[:].indirect(offs2_sb[:]), z_sb[:])
         res = keep.tile([P, T], F32, name="res")
-        for cols in (slice(0, T - P), slice(T - P, T)):
+        for cols in (slice(0, hT), slice(hT, T)):
             nc.vector.tensor_tensor(res[:, cols], back[:, cols], placed[:, cols], ADD)
             nc.sync.dma_start(out[:, cols], res[:, cols])

@@ -7,7 +7,12 @@ K, T, E, C, F, D, H, N, TOP = 512, 512, 6, 256, 2, 256, 512, 128, 3
 S = E * C
 A = F * D
 P = 128
-WINDOW = 1024
+BANK = 512
+PER_COLUMN = 16
+WINDOW = 2 * T
+WORD_CUTS = (0, 768, S)
+SCALE_CUTS = (0, 768, 1152, 1408, S)
+LAST_TERM_CUTS = (0, 256, 384, T)
 FLOPS = 2 * K * N * S + 2 * K * H * A + 2 * H * N * A
 
 F32 = mybir.dt.float32
@@ -24,6 +29,10 @@ COPY = mybir.ActivationFunctionType.Copy
 SILU = mybir.ActivationFunctionType.Silu
 
 
+def pieces(cuts):
+    return list(zip(cuts[:-1], cuts[1:]))
+
+
 def tile_moe_mlr_silu_kernel(
     tc, x_words, x_scales, w_words, w_scales, wa_words, wa_scales, wb_words, wb_scales,
     gate, gate2, offs, pos1, pos2, pos3, offs2, out,
@@ -32,24 +41,29 @@ def tile_moe_mlr_silu_kernel(
     with ExitStack() as ctx:
         keep = ctx.enter_context(tc.tile_pool(name="keep", bufs=1))
         stage = ctx.enter_context(tc.tile_pool(name="stage", bufs=2))
-        ps_h = ctx.enter_context(tc.psum_pool(name="ps_h", bufs=2))
-        ps_t = ctx.enter_context(tc.psum_pool(name="ps_t", bufs=3))
-        ps_y = ctx.enter_context(tc.psum_pool(name="ps_y", bufs=2))
-        ps_z = ctx.enter_context(tc.psum_pool(name="ps_z", bufs=1))
+        ring_a = ctx.enter_context(tc.psum_pool(name="ring_a", bufs=2))
+        ring_b = ctx.enter_context(tc.psum_pool(name="ring_b", bufs=3))
+        ring_c = ctx.enter_context(tc.psum_pool(name="ring_c", bufs=2))
+        ring_d = ctx.enter_context(tc.psum_pool(name="ring_d", bufs=1))
 
         def load_list(name, src):
-            t = keep.tile([P, src.shape[1]], U16, name=name)
-            nc.sync.dma_start(t[:], src)
-            return t
+            offsets = keep.tile([P, src.shape[1]], U16, name=name)
+            nc.sync.dma_start(offsets[:], src)
+            return offsets
 
-        def load_words(name, src, queue):
+        def load_fp4_words(name, src, queue):
             count, width = src.shape[0], src.shape[3]
-            t = keep.tile([P, count * width], U8, name=name, align_bytes=64)
+            words = keep.tile([P, count * width], U8, name=name, align_bytes=64)
             queue.dma_start(
-                t[:].bitcast(I32).rearrange("p (e w) -> p e w", e=count),
+                words[:].bitcast(I32).rearrange("p (e w) -> p e w", e=count),
                 src[:, 0].bitcast(I32).rearrange("e p w -> p e w"),
             )
-            return t
+            return words
+
+        def zeroed_plane(name, width, engine):
+            plane = keep.tile([P, width], U8, name=name, align_bytes=64)
+            engine.memset(plane[:].bitcast(I32), 0)
+            return plane
 
         def load_plane(plane, src):
             count, width = src.shape[0], src.shape[2]
@@ -59,32 +73,34 @@ def tile_moe_mlr_silu_kernel(
                     src[:, r:16:4, :].bitcast(I32).rearrange("e q w -> q e w"),
                 )
 
-        def zeroed_plane(name, width):
-            t = keep.tile([P, width], U8, name=name, align_bytes=64)
-            nc.vector.memset(t[:].bitcast(I32), 0)
-            return t
+        def entries(offsets, lo, hi):
+            return offsets[:, lo // PER_COLUMN : hi // PER_COLUMN]
 
-        tok_words = keep.tile([P, WINDOW], I32, name="tok_words", align_bytes=64)
-        nc.sync.dma_start(tok_words[:, 0:T], x_words[0].rearrange("p t d -> p (t d)").bitcast(I32))
-        tok_scales = zeroed_plane("tok_scales", WINDOW)
-        wa_plane = zeroed_plane("wa_plane", F * H)
-        w_plane = zeroed_plane("w_plane", E * N)
-        wb_plane = zeroed_plane("wb_plane", F * N)
-        nc.vector.memset(tok_words[:, T:WINDOW], 0)
+        def fp4_matrix(words, plane, index, width):
+            return words[:, 2 * index * width : 2 * (index + 1) * width].bitcast(FP4X4), plane[:, index * width : (index + 1) * width]
 
-        warm = keep.tile([P, 8], F32, name="warm")
-        nc.gpsimd.memset(warm[:], 0.0)
-        nc.scalar.activation(warm[:, 4:5], warm[:, 0:1], SILU)
-        ident32 = keep.tile([P, P], F32, name="ident32")
-        make_identity(nc, ident32[:])
+        token_words = keep.tile([P, WINDOW], I32, name="token_words", align_bytes=64)
+        nc.sync.dma_start(token_words[:, 0:T], x_words[0].rearrange("p t d -> p (t d)").bitcast(I32))
+        token_plane = zeroed_plane("token_plane", WINDOW, nc.vector)
+        nc.vector.memset(token_words[:, T:WINDOW], 0)
+
+        zeros = keep.tile([P, 8], F32, name="zeros")
+        nc.gpsimd.memset(zeros[:], 0.0)
+        zero_bias = zeros[:, 4:5]
+        nc.scalar.activation(zero_bias, zeros[:, 0:1], SILU)
+        wa_plane = zeroed_plane("wa_plane", F * H, nc.gpsimd)
+        identity = keep.tile([P, P], F32, name="identity")
+        make_identity(nc, identity[:])
+        w_plane = zeroed_plane("w_plane", E * N, nc.gpsimd)
+        wb_plane = zeroed_plane("wb_plane", F * N, nc.gpsimd)
 
         offs2_sb = load_list("offs2_sb", offs2)
-        load_plane(tok_scales, x_scales)
-        wa_sb = load_words("wa_sb", wa_words, nc.sync)
+        load_plane(token_plane, x_scales)
+        wa_sb = load_fp4_words("wa_sb", wa_words, nc.sync)
         offs_sb = load_list("offs_sb", offs)
         load_plane(wa_plane, wa_scales[:, 0])
-        w_sb = load_words("w_sb", w_words, nc.gpsimd)
-        wb_sb = load_words("wb_sb", wb_words, nc.gpsimd)
+        w_sb = load_fp4_words("w_sb", w_words, nc.gpsimd)
+        wb_sb = load_fp4_words("wb_sb", wb_words, nc.gpsimd)
         load_plane(w_plane, w_scales[:, 0])
         gate_sb = keep.tile([P, TOP, T], F32, name="gate_sb")
         nc.sync.dma_start(gate_sb[:], gate.rearrange("r p t -> p r t"))
@@ -94,122 +110,112 @@ def tile_moe_mlr_silu_kernel(
             nc.sync.dma_start(slot_gate[:], gate2[0].rearrange("(b m) -> m b", m=P))
         pos_sb = [load_list("pos1_sb", pos1), load_list("pos2_sb", pos2), load_list("pos3_sb", pos3)]
 
-        word_window = tok_words[:].bitcast(U32)
+        word_window = token_words[:].bitcast(U32)
 
         a_words = keep.tile([P, A], U32, name="a_words", align_bytes=64)
-        a_scales = keep.tile([P, A], U8, name="a_scales", align_bytes=64)
+        a_plane = keep.tile([P, A], U8, name="a_plane", align_bytes=64)
         nc.vector.tensor_copy(a_words[:], word_window.indirect(offs2_sb[:]))
-        nc.vector.tensor_copy(a_scales[:], tok_scales[:].indirect(offs2_sb[:]))
+        nc.vector.tensor_copy(a_plane[:], token_plane[:].indirect(offs2_sb[:]))
 
         h_grouped = keep.tile([P, A, 4], BF16, name="h_grouped", align_bytes=64)
         for b in range(A // P):
-            f = b * P // D
             slots = slice(b * P, (b + 1) * P)
-            pre = ps_h.tile([P, H], F32, name="pre")
+            wa_codes, wa_bytes = fp4_matrix(wa_sb, wa_plane, b * P // D, H)
+            pre = ring_a.tile([P, H], F32, name="pre", tag="a")
             nc.tensor.matmul_mx(
-                out=pre[:],
-                lhsT=a_words[:, slots].bitcast(FP8X4), lhsT_scale=a_scales[:, slots],
-                rhs=wa_sb[:, 2 * f * H : 2 * (f + 1) * H].bitcast(FP4X4), rhs_scale=wa_plane[:, f * H : (f + 1) * H],
-                start=True, stop=True,
+                out=pre[:], lhsT=a_words[:, slots].bitcast(FP8X4), lhsT_scale=a_plane[:, slots],
+                rhs=wa_codes, rhs_scale=wa_bytes, start=True, stop=True,
             )
             act = stage.tile([P, 2, P, 2], BF16, name="act")
-            nc.scalar.activation(act[:], pre[:].rearrange("m (q u v) -> m u q v", u=2, v=2), SILU)
+            nc.scalar.activation(act[:], pre[:].rearrange("m (q u v) -> m u q v", u=2, v=2), SILU, bias=zero_bias)
             pairs = act[:].rearrange("m u q v -> m (u q v)").bitcast(F32)
-            turned = ps_t.tile([P, 2, P], F32, name="turned")
+            turned = ring_b.tile([P, 2, P], F32, name="turned", tag="b")
             for u in range(2):
-                nc.tensor.transpose(turned[:, u, :], pairs[:, u * P : (u + 1) * P], ident32[:])
+                nc.tensor.transpose(turned[:, u, :], pairs[:, u * P : (u + 1) * P], identity[:])
             nc.scalar.copy(
                 h_grouped[:, slots, :].rearrange("q m t -> q (m t)").bitcast(F32).rearrange("q (m u) -> q m u", u=2),
                 turned[:].rearrange("q u m -> q m u"),
             )
 
         e_words = keep.tile([P, S], U32, name="e_words", align_bytes=64)
-        e_scales = keep.tile([P, S], U8, name="e_scales", align_bytes=64)
+        e_plane = keep.tile([P, S], U8, name="e_plane", align_bytes=64)
         y_sb = keep.tile([P, S], F32, name="y_sb")
 
-        def gather_slots(dst, window, lo, hi):
-            nc.vector.tensor_copy(dst[:, lo:hi], window.indirect(offs_sb[:, lo // 16 : hi // 16]))
-
         def experts(lo, hi):
-            bank = ps_t.tile([P, 2 * C], F32, name="turned")
+            y_bank = ring_b.tile([P, BANK], F32, name="y_bank", tag="b")
             for e in range(lo // C, (hi - 1) // C + 1):
                 slots = slice(max(lo, e * C), min(hi, (e + 1) * C))
+                w_codes, w_bytes = fp4_matrix(w_sb, w_plane, e, N)
                 nc.tensor.matmul_mx(
-                    out=bank[:, slots.start - lo : slots.stop - lo],
-                    lhsT=w_sb[:, 2 * e * N : 2 * (e + 1) * N].bitcast(FP4X4), lhsT_scale=w_plane[:, e * N : (e + 1) * N],
-                    rhs=e_words[:, slots].bitcast(FP8X4), rhs_scale=e_scales[:, slots],
-                    start=True, stop=True,
+                    out=y_bank[:, slots.start - lo : slots.stop - lo], lhsT=w_codes, lhsT_scale=w_bytes,
+                    rhs=e_words[:, slots].bitcast(FP8X4), rhs_scale=e_plane[:, slots], start=True, stop=True,
                 )
-            nc.scalar.copy(y_sb[:, lo:hi], bank[:, 0 : hi - lo])
+            nc.scalar.copy(y_sb[:, lo:hi], y_bank[:, 0 : hi - lo])
 
-        gather_slots(e_words, word_window, 0, 768)
-        gather_slots(e_words, word_window, 768, S)
-        gather_slots(e_scales, tok_scales[:], 0, 768)
-        experts(0, 512)
-        experts(512, 768)
-        gather_slots(e_scales, tok_scales[:], 768, 1152)
-        experts(768, 1152)
-        gather_slots(e_scales, tok_scales[:], 1152, 1408)
-        experts(1152, 1408)
-        gather_slots(e_scales, tok_scales[:], 1408, S)
-        experts(1408, S)
+        for lo, hi in pieces(WORD_CUTS):
+            nc.vector.tensor_copy(e_words[:, lo:hi], word_window.indirect(entries(offs_sb, lo, hi)))
+        for lo, hi in pieces(SCALE_CUTS):
+            nc.vector.tensor_copy(e_plane[:, lo:hi], token_plane[:].indirect(entries(offs_sb, lo, hi)))
+            for start in range(lo, hi, BANK):
+                experts(start, min(hi, start + BANK))
 
         h_codes = keep.tile([P, A], U32, name="h_codes", align_bytes=64)
         h_plane = keep.tile([P, A], U8, name="h_plane", align_bytes=64)
         nc.vector.quantize_mx(
             out=h_codes[:].bitcast(FP8X4), scales=h_plane[:], in_=h_grouped[:].rearrange("q m t -> q (m t)")
         )
-        z_bank = ps_z.tile([P, A // P, N], F32, name="z_bank")
+        blocks = D // P
+        z_banks = [
+            ring_d.tile([P, blocks, N], F32, name="z_bank0", tag="d"),
+            ring_a.tile([P, blocks, N], F32, name="z_bank1", tag="a"),
+        ]
         z_gated = keep.tile([P, A // P, N], F32, name="z_gated")
         for b in range(A // P):
-            f = b * P // D
             slots = slice(b * P, (b + 1) * P)
+            wb_codes, wb_bytes = fp4_matrix(wb_sb, wb_plane, b // blocks, N)
             nc.tensor.matmul_mx(
-                out=z_bank[:, b, :],
+                out=z_banks[b // blocks][:, b % blocks, :],
                 lhsT=h_codes[:, slots].bitcast(FP8X4), lhsT_scale=h_plane[:, slots],
-                rhs=wb_sb[:, 2 * f * N : 2 * (f + 1) * N].bitcast(FP4X4), rhs_scale=wb_plane[:, f * N : (f + 1) * N],
-                start=True, stop=True,
+                rhs=wb_codes, rhs_scale=wb_bytes, start=True, stop=True,
             )
         for b in range(A // P):
-            nc.scalar.activation(z_gated[:, b, :], z_bank[:, b, :], COPY, scale=slot_gate[:, b : b + 1])
-        z_back = ps_h.tile([P, H], F32, name="pre")
+            nc.scalar.activation(
+                z_gated[:, b, :], z_banks[b // blocks][:, b % blocks, :], COPY, scale=slot_gate[:, b : b + 1]
+            )
+        z_back = ring_a.tile([P, A], F32, name="z_back", tag="a")
         for b in range(A // P):
-            nc.tensor.transpose(z_back[:, b * P : (b + 1) * P], z_gated[:, b, :], ident32[:])
+            nc.tensor.transpose(z_back[:, b * P : (b + 1) * P], z_gated[:, b, :], identity[:])
         z_sb = keep.tile([P, A], F32, name="z_sb")
         nc.scalar.copy(z_sb[:], z_back[:])
 
         terms = keep.tile([P, TOP, T], F32, name="terms")
-        hT = T // 2
-        sums = [ps_t.tile([P, P], F32, name="turned") for b in range(2)] + [ps_y.tile([P, P], F32, name="bank") for b in range(2)]
+        sums = [ring_b.tile([P, N], F32, name="sum_b", tag="b") for b in range(2)]
+        sums = sums + [ring_c.tile([P, N], F32, name="sum_c", tag="c") for b in range(2)]
         sums_sb = keep.tile([P, T // P, N], F32, name="sums_sb")
-        back = ps_h.tile([P, T], F32, name="pre")
+        o_bank = ring_d.tile([P, T], F32, name="o_bank", tag="d")
 
         def term(r, lo, hi):
             nc.vector.tensor_tensor(
-                terms[:, r, lo:hi], y_sb[:].indirect(pos_sb[r][:, lo // 16 : hi // 16]), gate_sb[:, r, lo:hi], MULT
+                terms[:, r, lo:hi], y_sb[:].indirect(entries(pos_sb[r], lo, hi)), gate_sb[:, r, lo:hi], MULT
             )
             for b in range(lo // P, hi // P):
                 nc.tensor.matmul(
-                    sums[b][:], terms[:, r, b * P : (b + 1) * P], ident32[:],
+                    sums[b][:], terms[:, r, b * P : (b + 1) * P], identity[:],
                     start=(r == 0), stop=(r == TOP - 1), is_transpose=True,
                 )
 
-        def turn_back(lo, hi):
+        for r in range(TOP - 1):
+            term(r, 0, T)
+        for lo, hi in pieces(LAST_TERM_CUTS):
+            term(TOP - 1, lo, hi)
             for b in range(lo // P, hi // P):
                 nc.scalar.copy(sums_sb[:, b, :], sums[b][:])
             for b in range(lo // P, hi // P):
-                nc.tensor.transpose(back[:, b * P : (b + 1) * P], sums_sb[:, b, :], ident32[:])
-
-        term(0, 0, T)
-        term(1, 0, T)
-        term(2, 0, hT)
-        turn_back(0, hT)
-        term(2, hT, T)
-        turn_back(hT, T)
+                nc.tensor.transpose(o_bank[:, b * P : (b + 1) * P], sums_sb[:, b, :], identity[:])
 
         placed = keep.tile([P, WINDOW], F32, name="placed")
         nc.vector.tensor_copy(placed[:].indirect(offs2_sb[:]), z_sb[:])
-        res = keep.tile([P, T], F32, name="res")
-        for cols in (slice(0, hT), slice(hT, T)):
-            nc.vector.tensor_tensor(res[:, cols], back[:, cols], placed[:, cols], ADD)
-            nc.sync.dma_start(out[:, cols], res[:, cols])
+        result = keep.tile([P, T], F32, name="result")
+        for lo, hi in pieces((0, T // 2, T)):
+            nc.vector.tensor_tensor(result[:, lo:hi], o_bank[:, lo:hi], placed[:, lo:hi], ADD)
+            nc.sync.dma_start(out[:, lo:hi], result[:, lo:hi])

@@ -10,9 +10,6 @@ P = 128
 BANK = 512
 PER_COLUMN = 16
 WINDOW = 2 * T
-WORD_CUTS = (0, 768, S)
-SCALE_CUTS = (0, 768, 1152, 1408, S)
-LAST_TERM_CUTS = (0, 256, 384, T)
 FLOPS = 2 * K * N * S + 2 * K * H * A + 2 * H * N * A
 
 F32 = mybir.dt.float32
@@ -25,7 +22,6 @@ FP8X4 = mybir.dt.float8_e4m3fn_x4
 FP4X4 = mybir.dt.float4_e2m1fn_x4
 MULT = mybir.AluOpType.mult
 ADD = mybir.AluOpType.add
-COPY = mybir.ActivationFunctionType.Copy
 SILU = mybir.ActivationFunctionType.Silu
 
 
@@ -41,10 +37,10 @@ def tile_moe_mlr_silu_kernel(
     with ExitStack() as ctx:
         keep = ctx.enter_context(tc.tile_pool(name="keep", bufs=1))
         stage = ctx.enter_context(tc.tile_pool(name="stage", bufs=2))
-        ring_a = ctx.enter_context(tc.psum_pool(name="ring_a", bufs=2))
-        ring_b = ctx.enter_context(tc.psum_pool(name="ring_b", bufs=3))
-        ring_c = ctx.enter_context(tc.psum_pool(name="ring_c", bufs=2))
-        ring_d = ctx.enter_context(tc.psum_pool(name="ring_d", bufs=1))
+        psum = ctx.enter_context(tc.psum_pool(name="psum", bufs=1))
+
+        def bank(number, name, shape):
+            return psum.tile(shape, F32, name=name, tag="bank%d" % number)
 
         def load_list(name, src):
             offsets = keep.tile([P, src.shape[1]], U16, name=name)
@@ -82,33 +78,33 @@ def tile_moe_mlr_silu_kernel(
         token_words = keep.tile([P, WINDOW], I32, name="token_words", align_bytes=64)
         nc.sync.dma_start(token_words[:, 0:T], x_words[0].rearrange("p t d -> p (t d)").bitcast(I32))
         token_plane = zeroed_plane("token_plane", WINDOW, nc.vector)
+        wa_plane = zeroed_plane("wa_plane", F * H, nc.vector)
         nc.vector.memset(token_words[:, T:WINDOW], 0)
+        wb_plane = zeroed_plane("wb_plane", F * N, nc.vector)
+        w_plane = zeroed_plane("w_plane", E * N, nc.vector)
 
         zeros = keep.tile([P, 8], F32, name="zeros")
         nc.gpsimd.memset(zeros[:], 0.0)
         zero_bias = zeros[:, 4:5]
         nc.scalar.activation(zero_bias, zeros[:, 0:1], SILU)
-        wa_plane = zeroed_plane("wa_plane", F * H, nc.gpsimd)
         identity = keep.tile([P, P], F32, name="identity")
         make_identity(nc, identity[:])
-        w_plane = zeroed_plane("w_plane", E * N, nc.gpsimd)
-        wb_plane = zeroed_plane("wb_plane", F * N, nc.gpsimd)
 
         offs2_sb = load_list("offs2_sb", offs2)
         load_plane(token_plane, x_scales)
         wa_sb = load_fp4_words("wa_sb", wa_words, nc.sync)
         offs_sb = load_list("offs_sb", offs)
         load_plane(wa_plane, wa_scales[:, 0])
-        w_sb = load_fp4_words("w_sb", w_words, nc.gpsimd)
-        wb_sb = load_fp4_words("wb_sb", wb_words, nc.gpsimd)
+        wb_sb = load_fp4_words("wb_sb", wb_words, nc.sync)
+        load_plane(wb_plane, wb_scales[:, 0])
+        w_sb = load_fp4_words("w_sb", w_words, nc.sync)
         load_plane(w_plane, w_scales[:, 0])
+        gate2_sb = [keep.tile([P, D], F32, name="gate2_sb%d" % f) for f in range(F)]
+        nc.sync.dma_start(gate2_sb[0][:], gate2[:, 0:D])
+        pos_sb = [load_list("pos1_sb", pos1), load_list("pos2_sb", pos2), load_list("pos3_sb", pos3)]
         gate_sb = keep.tile([P, TOP, T], F32, name="gate_sb")
         nc.sync.dma_start(gate_sb[:], gate.rearrange("r p t -> p r t"))
-        load_plane(wb_plane, wb_scales[:, 0])
-        slot_gate = keep.tile([P, A // P], F32, name="slot_gate")
-        with nc.allow_non_contiguous_dma(reason="one weight a partition"):
-            nc.sync.dma_start(slot_gate[:], gate2[0].rearrange("(b m) -> m b", m=P))
-        pos_sb = [load_list("pos1_sb", pos1), load_list("pos2_sb", pos2), load_list("pos3_sb", pos3)]
+        nc.sync.dma_start(gate2_sb[1][:], gate2[:, D:A])
 
         word_window = token_words[:].bitcast(U32)
 
@@ -117,11 +113,11 @@ def tile_moe_mlr_silu_kernel(
         nc.vector.tensor_copy(a_words[:], word_window.indirect(offs2_sb[:]))
         nc.vector.tensor_copy(a_plane[:], token_plane[:].indirect(offs2_sb[:]))
 
-        h_grouped = keep.tile([P, A, 4], BF16, name="h_grouped", align_bytes=64)
+        h_grouped = [keep.tile([P, D, 4], BF16, name="h_grouped", tag="h_grouped%d" % f, align_bytes=64) for f in range(F)]
         for b in range(A // P):
             slots = slice(b * P, (b + 1) * P)
             wa_codes, wa_bytes = fp4_matrix(wa_sb, wa_plane, b * P // D, H)
-            pre = ring_a.tile([P, H], F32, name="pre", tag="a")
+            pre = bank(b % 2, "pre", [P, H])
             nc.tensor.matmul_mx(
                 out=pre[:], lhsT=a_words[:, slots].bitcast(FP8X4), lhsT_scale=a_plane[:, slots],
                 rhs=wa_codes, rhs_scale=wa_bytes, start=True, stop=True,
@@ -129,70 +125,78 @@ def tile_moe_mlr_silu_kernel(
             act = stage.tile([P, 2, P, 2], BF16, name="act")
             nc.scalar.activation(act[:], pre[:].rearrange("m (q u v) -> m u q v", u=2, v=2), SILU, bias=zero_bias)
             pairs = act[:].rearrange("m u q v -> m (u q v)").bitcast(F32)
-            turned = ring_b.tile([P, 2, P], F32, name="turned", tag="b")
+            turned = bank(2 + b % 2, "turned", [P, 2, P])
             for u in range(2):
                 nc.tensor.transpose(turned[:, u, :], pairs[:, u * P : (u + 1) * P], identity[:])
             nc.scalar.copy(
-                h_grouped[:, slots, :].rearrange("q m t -> q (m t)").bitcast(F32).rearrange("q (m u) -> q m u", u=2),
+                h_grouped[b * P // D][:, b * P % D : b * P % D + P, :].rearrange("q m t -> q (m t)").bitcast(F32).rearrange("q (m u) -> q m u", u=2),
                 turned[:].rearrange("q u m -> q m u"),
             )
 
+        half = S // 2
         e_words = keep.tile([P, S], U32, name="e_words", align_bytes=64)
-        e_plane = keep.tile([P, S], U8, name="e_plane", align_bytes=64)
-        y_sb = keep.tile([P, S], F32, name="y_sb")
-
-        def experts(lo, hi):
-            y_bank = ring_b.tile([P, BANK], F32, name="y_bank", tag="b")
-            for e in range(lo // C, (hi - 1) // C + 1):
-                slots = slice(max(lo, e * C), min(hi, (e + 1) * C))
-                w_codes, w_bytes = fp4_matrix(w_sb, w_plane, e, N)
-                nc.tensor.matmul_mx(
-                    out=y_bank[:, slots.start - lo : slots.stop - lo], lhsT=w_codes, lhsT_scale=w_bytes,
-                    rhs=e_words[:, slots].bitcast(FP8X4), rhs_scale=e_plane[:, slots], start=True, stop=True,
-                )
-            nc.scalar.copy(y_sb[:, lo:hi], y_bank[:, 0 : hi - lo])
-
-        for lo, hi in pieces(WORD_CUTS):
-            nc.vector.tensor_copy(e_words[:, lo:hi], word_window.indirect(entries(offs_sb, lo, hi)))
-        for lo, hi in pieces(SCALE_CUTS):
-            nc.vector.tensor_copy(e_plane[:, lo:hi], token_plane[:].indirect(entries(offs_sb, lo, hi)))
-            for start in range(lo, hi, BANK):
-                experts(start, min(hi, start + BANK))
-
-        h_codes = keep.tile([P, A], U32, name="h_codes", align_bytes=64)
+        h_codes = [keep.tile([P, D], U32, name="h_codes", tag="h_codes%d" % f, align_bytes=64) for f in range(F)]
         h_plane = keep.tile([P, A], U8, name="h_plane", align_bytes=64)
-        nc.vector.quantize_mx(
-            out=h_codes[:].bitcast(FP8X4), scales=h_plane[:], in_=h_grouped[:].rearrange("q m t -> q (m t)")
-        )
-        blocks = D // P
-        z_banks = [
-            ring_d.tile([P, blocks, N], F32, name="z_bank0", tag="d"),
-            ring_a.tile([P, blocks, N], F32, name="z_bank1", tag="a"),
-        ]
-        z_gated = keep.tile([P, A // P, N], F32, name="z_gated")
-        for b in range(A // P):
-            slots = slice(b * P, (b + 1) * P)
-            wb_codes, wb_bytes = fp4_matrix(wb_sb, wb_plane, b // blocks, N)
-            nc.tensor.matmul_mx(
-                out=z_banks[b // blocks][:, b % blocks, :],
-                lhsT=h_codes[:, slots].bitcast(FP8X4), lhsT_scale=h_plane[:, slots],
-                rhs=wb_codes, rhs_scale=wb_bytes, start=True, stop=True,
-            )
-        for b in range(A // P):
-            nc.scalar.activation(
-                z_gated[:, b, :], z_banks[b // blocks][:, b % blocks, :], COPY, scale=slot_gate[:, b : b + 1]
-            )
-        z_back = ring_a.tile([P, A], F32, name="z_back", tag="a")
-        for b in range(A // P):
-            nc.tensor.transpose(z_back[:, b * P : (b + 1) * P], z_gated[:, b, :], identity[:])
         z_sb = keep.tile([P, A], F32, name="z_sb")
-        nc.scalar.copy(z_sb[:], z_back[:])
+        placed = keep.tile([P, T], F32, name="placed")
+
+        def quantise(f):
+            nc.vector.quantize_mx(
+                out=h_codes[f][:].bitcast(FP8X4), scales=h_plane[:, f * D : (f + 1) * D],
+                in_=h_grouped[f][:].rearrange("q m t -> q (m t)"),
+            )
+
+        def adapter(f):
+            slots = slice(f * D, (f + 1) * D)
+            wb_codes, wb_bytes = fp4_matrix(wb_sb, wb_plane, f, N)
+            z_bank = bank(6, "z_bank", [P, D])
+            nc.tensor.matmul_mx(
+                out=z_bank[:], lhsT=wb_codes, lhsT_scale=wb_bytes,
+                rhs=h_codes[f][:].bitcast(FP8X4), rhs_scale=h_plane[:, slots], start=True, stop=True,
+            )
+            nc.scalar.copy(z_sb[:, slots], z_bank[:])
+
+        def scatter(f):
+            slots = slice(f * D, (f + 1) * D)
+            nc.vector.tensor_tensor(
+                placed[:].indirect(entries(offs2_sb, slots.start, slots.stop)), z_sb[:, slots], gate2_sb[f][:], MULT
+            )
+
+        nc.vector.tensor_copy(e_words[:, 0:half], word_window.indirect(entries(offs_sb, 0, half)))
+        first_plane = keep.tile([P, half], U8, name="first_plane", align_bytes=64)
+        nc.vector.tensor_copy(first_plane[:], token_plane[:].indirect(entries(offs_sb, 0, half)))
+        nc.vector.tensor_copy(e_words[:, half:S], word_window.indirect(entries(offs_sb, half, S)))
+        quantise(0)
+        second_plane = keep.tile([P, half], U8, name="second_plane", tag="h_grouped0", align_bytes=64)
+        nc.vector.tensor_copy(second_plane[:], token_plane[:].indirect(entries(offs_sb, half, S)))
+        adapter(0)
+
+        y_sb = keep.tile([P, S], F32, name="y_sb", tag="h_codes0", align_bytes=64)
+
+        def experts(first, count, plane, number):
+            y_bank = bank(number, "y_bank", [P, count * C])
+            for e in range(first, first + count):
+                w_codes, w_bytes = fp4_matrix(w_sb, w_plane, e, N)
+                at = e * C % half
+                nc.tensor.matmul_mx(
+                    out=y_bank[:, (e - first) * C : (e - first + 1) * C], lhsT=w_codes, lhsT_scale=w_bytes,
+                    rhs=e_words[:, e * C : (e + 1) * C].bitcast(FP8X4), rhs_scale=plane[:, at : at + C],
+                    start=True, stop=True,
+                )
+            nc.scalar.copy(y_sb[:, first * C : (first + count) * C], y_bank[:])
+
+        experts(0, 2, first_plane, 0)
+        experts(2, 1, first_plane, 1)
+        experts(3, 2, second_plane, 3)
+        experts(5, 1, second_plane, 6)
+        scatter(0)
+        quantise(1)
+        adapter(1)
 
         terms = keep.tile([P, TOP, T], F32, name="terms")
-        sums = [ring_b.tile([P, N], F32, name="sum_b", tag="b") for b in range(2)]
-        sums = sums + [ring_c.tile([P, N], F32, name="sum_c", tag="c") for b in range(2)]
+        sums = [bank(b, "sums", [P, N]) for b in range(T // P)]
         sums_sb = keep.tile([P, T // P, N], F32, name="sums_sb")
-        o_bank = ring_d.tile([P, T], F32, name="o_bank", tag="d")
+        o_bank = bank(4, "o_bank", [P, T])
 
         def term(r, lo, hi):
             nc.vector.tensor_tensor(
@@ -206,15 +210,14 @@ def tile_moe_mlr_silu_kernel(
 
         for r in range(TOP - 1):
             term(r, 0, T)
-        for lo, hi in pieces(LAST_TERM_CUTS):
+        for lo, hi in pieces((0, T // 2, T)):
             term(TOP - 1, lo, hi)
             for b in range(lo // P, hi // P):
                 nc.scalar.copy(sums_sb[:, b, :], sums[b][:])
             for b in range(lo // P, hi // P):
                 nc.tensor.transpose(o_bank[:, b * P : (b + 1) * P], sums_sb[:, b, :], identity[:])
+        scatter(1)
 
-        placed = keep.tile([P, WINDOW], F32, name="placed")
-        nc.vector.tensor_copy(placed[:].indirect(offs2_sb[:]), z_sb[:])
         result = keep.tile([P, T], F32, name="result")
         for lo, hi in pieces((0, T // 2, T)):
             nc.vector.tensor_tensor(result[:, lo:hi], o_bank[:, lo:hi], placed[:, lo:hi], ADD)

@@ -10,6 +10,7 @@ P = 128
 BANK = 512
 PER_COLUMN = 16
 WINDOW = 2 * T
+SCATTER_CUTS = (0, D, A)
 FLOPS = 2 * K * N * S + 2 * K * H * A + 2 * H * N * A
 
 F32 = mybir.dt.float32
@@ -36,7 +37,6 @@ def tile_moe_mlr_silu_kernel(
     nc = tc.nc
     with ExitStack() as ctx:
         keep = ctx.enter_context(tc.tile_pool(name="keep", bufs=1))
-        stage = ctx.enter_context(tc.tile_pool(name="stage", bufs=2))
         psum = ctx.enter_context(tc.psum_pool(name="psum", bufs=1))
 
         def bank(number, name, shape):
@@ -99,12 +99,12 @@ def tile_moe_mlr_silu_kernel(
         load_plane(wb_plane, wb_scales[:, 0])
         w_sb = load_fp4_words("w_sb", w_words, nc.sync)
         load_plane(w_plane, w_scales[:, 0])
-        gate2_sb = [keep.tile([P, D], F32, name="gate2_sb%d" % f) for f in range(F)]
-        nc.sync.dma_start(gate2_sb[0][:], gate2[:, 0:D])
+        gate2_sb = [keep.tile([P, hi - lo], F32, name="gate2_sb%d" % lo) for lo, hi in pieces(SCATTER_CUTS)]
+        nc.sync.dma_start(gate2_sb[0][:], gate2[:, 0 : SCATTER_CUTS[1]])
         pos_sb = [load_list("pos1_sb", pos1), load_list("pos2_sb", pos2), load_list("pos3_sb", pos3)]
         gate_sb = keep.tile([P, TOP, T], F32, name="gate_sb")
         nc.sync.dma_start(gate_sb[:], gate.rearrange("r p t -> p r t"))
-        nc.sync.dma_start(gate2_sb[1][:], gate2[:, D:A])
+        nc.sync.dma_start(gate2_sb[1][:], gate2[:, SCATTER_CUTS[1] : A])
 
         word_window = token_words[:].bitcast(U32)
 
@@ -122,7 +122,7 @@ def tile_moe_mlr_silu_kernel(
                 out=pre[:], lhsT=a_words[:, slots].bitcast(FP8X4), lhsT_scale=a_plane[:, slots],
                 rhs=wa_codes, rhs_scale=wa_bytes, start=True, stop=True,
             )
-            act = stage.tile([P, 2, P, 2], BF16, name="act")
+            act = keep.tile([P, 2, P, 2], BF16, name="act", tag="act%d" % (b % 2), align_bytes=64)
             nc.scalar.activation(act[:], pre[:].rearrange("m (q u v) -> m u q v", u=2, v=2), SILU, bias=zero_bias)
             pairs = act[:].rearrange("m u q v -> m (u q v)").bitcast(F32)
             turned = bank(2 + b % 2, "turned", [P, 2, P])
@@ -156,19 +156,18 @@ def tile_moe_mlr_silu_kernel(
             )
             nc.scalar.copy(z_sb[:, slots], z_bank[:])
 
-        def scatter(f):
-            slots = slice(f * D, (f + 1) * D)
-            nc.vector.tensor_tensor(
-                placed[:].indirect(entries(offs2_sb, slots.start, slots.stop)), z_sb[:, slots], gate2_sb[f][:], MULT
-            )
+        def scatter(part):
+            lo, hi = pieces(SCATTER_CUTS)[part]
+            nc.vector.tensor_tensor(placed[:].indirect(entries(offs2_sb, lo, hi)), z_sb[:, lo:hi], gate2_sb[part][:], MULT)
 
         nc.vector.tensor_copy(e_words[:, 0:half], word_window.indirect(entries(offs_sb, 0, half)))
         first_plane = keep.tile([P, half], U8, name="first_plane", align_bytes=64)
         nc.vector.tensor_copy(first_plane[:], token_plane[:].indirect(entries(offs_sb, 0, half)))
         nc.vector.tensor_copy(e_words[:, half:S], word_window.indirect(entries(offs_sb, half, S)))
         quantise(0)
-        second_plane = keep.tile([P, half], U8, name="second_plane", tag="h_grouped0", align_bytes=64)
-        nc.vector.tensor_copy(second_plane[:], token_plane[:].indirect(entries(offs_sb, half, S)))
+        second_plane = keep.tile([P, half], U8, name="second_plane", tag="act0", align_bytes=64)
+        for lo, hi in pieces((half, S - C, S)):
+            nc.vector.tensor_copy(second_plane[:, lo - half : hi - half], token_plane[:].indirect(entries(offs_sb, lo, hi)))
         adapter(0)
 
         y_sb = keep.tile([P, S], F32, name="y_sb", tag="h_codes0", align_bytes=64)
@@ -196,7 +195,7 @@ def tile_moe_mlr_silu_kernel(
         terms = keep.tile([P, TOP, T], F32, name="terms")
         sums = [bank(b, "sums", [P, N]) for b in range(T // P)]
         sums_sb = keep.tile([P, T // P, N], F32, name="sums_sb")
-        o_bank = bank(4, "o_bank", [P, T])
+        o_banks = [bank(4 + part, "o_bank", [P, T // 2]) for part in range(2)]
 
         def term(r, lo, hi):
             nc.vector.tensor_tensor(
@@ -215,10 +214,10 @@ def tile_moe_mlr_silu_kernel(
             for b in range(lo // P, hi // P):
                 nc.scalar.copy(sums_sb[:, b, :], sums[b][:])
             for b in range(lo // P, hi // P):
-                nc.tensor.transpose(o_bank[:, b * P : (b + 1) * P], sums_sb[:, b, :], identity[:])
+                nc.tensor.transpose(o_banks[b // 2][:, b % 2 * P : (b % 2 + 1) * P], sums_sb[:, b, :], identity[:])
         scatter(1)
 
         result = keep.tile([P, T], F32, name="result")
         for lo, hi in pieces((0, T // 2, T)):
-            nc.vector.tensor_tensor(result[:, lo:hi], o_bank[:, lo:hi], placed[:, lo:hi], ADD)
+            nc.vector.tensor_tensor(result[:, lo:hi], o_banks[2 * lo // T][:], placed[:, lo:hi], ADD)
             nc.sync.dma_start(out[:, lo:hi], result[:, lo:hi])

@@ -10,6 +10,7 @@ P = 128
 BANK = 512
 PER_COLUMN = 16
 WINDOW = 2 * T
+WORD_WINDOW = 4 * T
 SCATTER_CUTS = (0, D, A)
 FLOPS = 2 * K * N * S + 2 * K * H * A + 2 * H * N * A
 
@@ -75,18 +76,14 @@ def tile_moe_mlr_silu_kernel(
         def fp4_matrix(words, plane, index, width):
             return words[:, 2 * index * width : 2 * (index + 1) * width].bitcast(FP4X4), plane[:, index * width : (index + 1) * width]
 
-        token_words = keep.tile([P, WINDOW], I32, name="token_words", align_bytes=64)
+        token_words = keep.tile([P, WORD_WINDOW], I32, name="token_words", align_bytes=64)
         nc.sync.dma_start(token_words[:, 0:T], x_words[0].rearrange("p t d -> p (t d)").bitcast(I32))
-        token_plane = zeroed_plane("token_plane", WINDOW, nc.vector)
+        token_plane = keep.tile([P, WINDOW], U8, name="token_plane", align_bytes=64)
+        nc.vector.memset(token_plane[:, 0:T].bitcast(I32), 0)
         wa_plane = zeroed_plane("wa_plane", F * H, nc.vector)
-        nc.vector.memset(token_words[:, T:WINDOW], 0)
         wb_plane = zeroed_plane("wb_plane", F * N, nc.vector)
         w_plane = zeroed_plane("w_plane", E * N, nc.vector)
 
-        zeros = keep.tile([P, 8], F32, name="zeros")
-        nc.gpsimd.memset(zeros[:], 0.0)
-        zero_bias = zeros[:, 4:5]
-        nc.scalar.activation(zero_bias, zeros[:, 0:1], SILU)
         identity = keep.tile([P, P], F32, name="identity")
         make_identity(nc, identity[:])
 
@@ -123,7 +120,7 @@ def tile_moe_mlr_silu_kernel(
                 rhs=wa_codes, rhs_scale=wa_bytes, start=True, stop=True,
             )
             act = keep.tile([P, 2, P, 2], BF16, name="act", tag="act%d" % (b % 2), align_bytes=64)
-            nc.scalar.activation(act[:], pre[:].rearrange("m (q u v) -> m u q v", u=2, v=2), SILU, bias=zero_bias)
+            nc.scalar.activation(act[:], pre[:].rearrange("m (q u v) -> m u q v", u=2, v=2), SILU)
             pairs = act[:].rearrange("m u q v -> m (u q v)").bitcast(F32)
             turned = bank(2 + b % 2, "turned", [P, 2, P])
             for u in range(2):
@@ -160,13 +157,12 @@ def tile_moe_mlr_silu_kernel(
             lo, hi = pieces(SCATTER_CUTS)[part]
             nc.vector.tensor_tensor(placed[:].indirect(entries(offs2_sb, lo, hi)), z_sb[:, lo:hi], gate2_sb[part][:], MULT)
 
-        nc.vector.tensor_copy(e_words[:, 0:half], word_window.indirect(entries(offs_sb, 0, half)))
+        nc.vector.tensor_copy(e_words[:], word_window.indirect(offs_sb[:]))
         first_plane = keep.tile([P, half], U8, name="first_plane", align_bytes=64)
         nc.vector.tensor_copy(first_plane[:], token_plane[:].indirect(entries(offs_sb, 0, half)))
-        nc.vector.tensor_copy(e_words[:, half:S], word_window.indirect(entries(offs_sb, half, S)))
         quantise(0)
         second_plane = keep.tile([P, half], U8, name="second_plane", tag="act0", align_bytes=64)
-        for lo, hi in pieces((half, S - C, S)):
+        for lo, hi in pieces((half, S)):
             nc.vector.tensor_copy(second_plane[:, lo - half : hi - half], token_plane[:].indirect(entries(offs_sb, lo, hi)))
         adapter(0)
 
@@ -186,7 +182,8 @@ def tile_moe_mlr_silu_kernel(
 
         experts(0, 2, first_plane, 0)
         experts(2, 1, first_plane, 1)
-        experts(3, 2, second_plane, 3)
+        experts(3, 1, second_plane, 3)
+        experts(4, 1, second_plane, 7)
         experts(5, 1, second_plane, 6)
         scatter(0)
         quantise(1)
@@ -195,7 +192,7 @@ def tile_moe_mlr_silu_kernel(
         terms = keep.tile([P, TOP, T], F32, name="terms")
         sums = [bank(b, "sums", [P, N]) for b in range(T // P)]
         sums_sb = keep.tile([P, T // P, N], F32, name="sums_sb")
-        o_banks = [bank(4 + part, "o_bank", [P, T // 2]) for part in range(2)]
+        o_banks = [bank(4 + b, "o_bank", [P, P]) for b in range(T // P)]
 
         def term(r, lo, hi):
             nc.vector.tensor_tensor(
@@ -207,17 +204,17 @@ def tile_moe_mlr_silu_kernel(
                     start=(r == 0), stop=(r == TOP - 1), is_transpose=True,
                 )
 
-        for r in range(TOP - 1):
+        for r in range(TOP):
             term(r, 0, T)
         for lo, hi in pieces((0, T // 2, T)):
-            term(TOP - 1, lo, hi)
             for b in range(lo // P, hi // P):
                 nc.scalar.copy(sums_sb[:, b, :], sums[b][:])
             for b in range(lo // P, hi // P):
-                nc.tensor.transpose(o_banks[b // 2][:, b % 2 * P : (b % 2 + 1) * P], sums_sb[:, b, :], identity[:])
+                nc.tensor.transpose(o_banks[b][:], sums_sb[:, b, :], identity[:])
         scatter(1)
 
         result = keep.tile([P, T], F32, name="result")
-        for lo, hi in pieces((0, T // 2, T)):
-            nc.vector.tensor_tensor(result[:, lo:hi], o_banks[2 * lo // T][:], placed[:, lo:hi], ADD)
-            nc.sync.dma_start(out[:, lo:hi], result[:, lo:hi])
+        for b in range(T // P):
+            tokens = slice(b * P, (b + 1) * P)
+            nc.vector.tensor_tensor(result[:, tokens], o_banks[b][:], placed[:, tokens], ADD)
+            (nc.scalar, nc.sync)[b % 2].dma_start(out[:, tokens], result[:, tokens])

@@ -78,7 +78,7 @@ def tile_moe_mlr_silu_kernel(
 
         token_words = keep.tile([P, WORD_WINDOW], I32, name="token_words", align_bytes=64)
         nc.sync.dma_start(token_words[:, 0:T], x_words[0].rearrange("p t d -> p (t d)").bitcast(I32))
-        token_plane = keep.tile([P, WINDOW], U8, name="token_plane", align_bytes=64)
+        token_plane = keep.tile([P, WORD_WINDOW], U8, name="token_plane", align_bytes=64)
         nc.vector.memset(token_plane[:, 0:T].bitcast(I32), 0)
         wa_plane = zeroed_plane("wa_plane", F * H, nc.vector)
         wb_plane = zeroed_plane("wb_plane", F * N, nc.vector)
@@ -111,18 +111,20 @@ def tile_moe_mlr_silu_kernel(
         nc.vector.tensor_copy(a_plane[:], token_plane[:].indirect(offs2_sb[:]))
 
         h_grouped = [keep.tile([P, D, 4], BF16, name="h_grouped", tag="h_grouped%d" % f, align_bytes=64) for f in range(F)]
-        for b in range(A // P):
+        blocks = range(A // P)
+        pre = [bank(b, "pre", [P, H]) for b in blocks]
+        act = [keep.tile([P, 2, P, 2], BF16, name="act", tag="act%d" % b, align_bytes=64) for b in blocks]
+        for b in blocks:
             slots = slice(b * P, (b + 1) * P)
             wa_codes, wa_bytes = fp4_matrix(wa_sb, wa_plane, b * P // D, H)
-            pre = bank(b % 2, "pre", [P, H])
             nc.tensor.matmul_mx(
-                out=pre[:], lhsT=a_words[:, slots].bitcast(FP8X4), lhsT_scale=a_plane[:, slots],
+                out=pre[b][:], lhsT=a_words[:, slots].bitcast(FP8X4), lhsT_scale=a_plane[:, slots],
                 rhs=wa_codes, rhs_scale=wa_bytes, start=True, stop=True,
             )
-            act = keep.tile([P, 2, P, 2], BF16, name="act", tag="act%d" % (b % 2), align_bytes=64)
-            nc.scalar.activation(act[:], pre[:].rearrange("m (q u v) -> m u q v", u=2, v=2), SILU)
-            pairs = act[:].rearrange("m u q v -> m (u q v)").bitcast(F32)
-            turned = bank(2 + b % 2, "turned", [P, 2, P])
+            nc.scalar.activation(act[b][:], pre[b][:].rearrange("m (q u v) -> m u q v", u=2, v=2), SILU)
+        for b in blocks:
+            pairs = act[b][:].rearrange("m u q v -> m (u q v)").bitcast(F32)
+            turned = bank((4, 5, 6, 5)[b], "turned", [P, 2, P])
             for u in range(2):
                 nc.tensor.transpose(turned[:, u, :], pairs[:, u * P : (u + 1) * P], identity[:])
             nc.scalar.copy(
@@ -130,7 +132,7 @@ def tile_moe_mlr_silu_kernel(
                 turned[:].rearrange("q u m -> q m u"),
             )
 
-        half = S // 2
+        half = 3 * C
         e_words = keep.tile([P, S], U32, name="e_words", align_bytes=64)
         h_codes = [keep.tile([P, D], U32, name="h_codes", tag="h_codes%d" % f, align_bytes=64) for f in range(F)]
         h_plane = keep.tile([P, A], U8, name="h_plane", align_bytes=64)
@@ -146,7 +148,7 @@ def tile_moe_mlr_silu_kernel(
         def adapter(f):
             slots = slice(f * D, (f + 1) * D)
             wb_codes, wb_bytes = fp4_matrix(wb_sb, wb_plane, f, N)
-            z_bank = bank(6, "z_bank", [P, D])
+            z_bank = bank((4, 7)[f], "z_bank", [P, D])
             nc.tensor.matmul_mx(
                 out=z_bank[:], lhsT=wb_codes, lhsT_scale=wb_bytes,
                 rhs=h_codes[f][:].bitcast(FP8X4), rhs_scale=h_plane[:, slots], start=True, stop=True,
@@ -161,30 +163,30 @@ def tile_moe_mlr_silu_kernel(
         first_plane = keep.tile([P, half], U8, name="first_plane", align_bytes=64)
         nc.vector.tensor_copy(first_plane[:], token_plane[:].indirect(entries(offs_sb, 0, half)))
         quantise(0)
-        second_plane = keep.tile([P, half], U8, name="second_plane", tag="act0", align_bytes=64)
-        for lo, hi in pieces((half, S)):
+        second_plane = keep.tile([P, S - half], U8, name="second_plane", tag="act3", align_bytes=64)
+        for lo, hi in pieces((half, S - C, S)):
             nc.vector.tensor_copy(second_plane[:, lo - half : hi - half], token_plane[:].indirect(entries(offs_sb, lo, hi)))
         adapter(0)
 
-        y_sb = keep.tile([P, S], F32, name="y_sb", tag="h_codes0", align_bytes=64)
+        y_sb = keep.tile([P, S], F32, name="y_sb")
 
-        def experts(first, count, plane, number):
-            y_bank = bank(number, "y_bank", [P, count * C])
-            for e in range(first, first + count):
-                w_codes, w_bytes = fp4_matrix(w_sb, w_plane, e, N)
-                at = e * C % half
+        def experts(lo, hi, number):
+            plane, base = (first_plane, 0) if lo < half else (second_plane, half)
+            y_bank = bank(number, "y_bank", [P, hi - lo])
+            for start, end in pieces([lo] + list(range(lo // C * C + C, hi, C)) + [hi]):
+                w_codes, w_bytes = fp4_matrix(w_sb, w_plane, start // C, N)
                 nc.tensor.matmul_mx(
-                    out=y_bank[:, (e - first) * C : (e - first + 1) * C], lhsT=w_codes, lhsT_scale=w_bytes,
-                    rhs=e_words[:, e * C : (e + 1) * C].bitcast(FP8X4), rhs_scale=plane[:, at : at + C],
+                    out=y_bank[:, start - lo : end - lo], lhsT=w_codes, lhsT_scale=w_bytes,
+                    rhs=e_words[:, start:end].bitcast(FP8X4), rhs_scale=plane[:, start - base : end - base],
                     start=True, stop=True,
                 )
-            nc.scalar.copy(y_sb[:, first * C : (first + count) * C], y_bank[:])
+            nc.scalar.copy(y_sb[:, lo:hi], y_bank[:])
 
-        experts(0, 2, first_plane, 0)
-        experts(2, 1, first_plane, 1)
-        experts(3, 1, second_plane, 3)
-        experts(4, 1, second_plane, 7)
-        experts(5, 1, second_plane, 6)
+        experts(0, C, 6)
+        experts(C, half, 5)
+        experts(half, 4 * C, 0)
+        experts(4 * C, 5 * C, 1)
+        experts(5 * C, S, 7)
         scatter(0)
         quantise(1)
         adapter(1)
@@ -204,9 +206,10 @@ def tile_moe_mlr_silu_kernel(
                     start=(r == 0), stop=(r == TOP - 1), is_transpose=True,
                 )
 
-        for r in range(TOP):
+        for r in range(TOP - 1):
             term(r, 0, T)
         for lo, hi in pieces((0, T // 2, T)):
+            term(TOP - 1, lo, hi)
             for b in range(lo // P, hi // P):
                 nc.scalar.copy(sums_sb[:, b, :], sums[b][:])
             for b in range(lo // P, hi // P):

@@ -7,11 +7,12 @@ K, T, E, C, F, D, H, N, TOP = 512, 512, 6, 256, 2, 256, 512, 128, 3
 S = E * C
 A = F * D
 P = 128
-BANK = 512
 PER_COLUMN = 16
-WINDOW = 2 * T
-WORD_WINDOW = 4 * T
-SCATTER_CUTS = (0, D, A)
+GATHER_WINDOW = 4 * T
+SCATTER_WINDOW = 2 * T
+PLANE_CUT = 3 * C
+LAST_EXPERT = S - C
+SCATTER_CUT = 224
 FLOPS = 2 * K * N * S + 2 * K * H * A + 2 * H * N * A
 
 F32 = mybir.dt.float32
@@ -48,18 +49,18 @@ def tile_moe_mlr_silu_kernel(
             nc.sync.dma_start(offsets[:], src)
             return offsets
 
-        def load_fp4_words(name, src, queue):
+        def load_fp4_words(name, src):
             count, width = src.shape[0], src.shape[3]
             words = keep.tile([P, count * width], U8, name=name, align_bytes=64)
-            queue.dma_start(
+            nc.sync.dma_start(
                 words[:].bitcast(I32).rearrange("p (e w) -> p e w", e=count),
                 src[:, 0].bitcast(I32).rearrange("e p w -> p e w"),
             )
             return words
 
-        def zeroed_plane(name, width, engine):
+        def zeroed_plane(name, width, loaded):
             plane = keep.tile([P, width], U8, name=name, align_bytes=64)
-            engine.memset(plane[:].bitcast(I32), 0)
+            nc.vector.memset(plane[:, 0:loaded].bitcast(I32), 0)
             return plane
 
         def load_plane(plane, src):
@@ -76,32 +77,32 @@ def tile_moe_mlr_silu_kernel(
         def fp4_matrix(words, plane, index, width):
             return words[:, 2 * index * width : 2 * (index + 1) * width].bitcast(FP4X4), plane[:, index * width : (index + 1) * width]
 
-        token_words = keep.tile([P, WORD_WINDOW], I32, name="token_words", align_bytes=64)
+        token_words = keep.tile([P, GATHER_WINDOW], I32, name="token_words", align_bytes=64)
         nc.sync.dma_start(token_words[:, 0:T], x_words[0].rearrange("p t d -> p (t d)").bitcast(I32))
-        token_plane = keep.tile([P, WORD_WINDOW], U8, name="token_plane", align_bytes=64)
-        nc.vector.memset(token_plane[:, 0:T].bitcast(I32), 0)
-        wa_plane = zeroed_plane("wa_plane", F * H, nc.vector)
-        wb_plane = zeroed_plane("wb_plane", F * N, nc.vector)
-        w_plane = zeroed_plane("w_plane", E * N, nc.vector)
+        token_plane = zeroed_plane("token_plane", GATHER_WINDOW, T)
+        wa_plane = zeroed_plane("wa_plane", F * H, F * H)
+        wb_plane = zeroed_plane("wb_plane", F * N, F * N)
+        w_plane = zeroed_plane("w_plane", E * N, E * N)
 
         identity = keep.tile([P, P], F32, name="identity")
         make_identity(nc, identity[:])
 
         offs2_sb = load_list("offs2_sb", offs2)
         load_plane(token_plane, x_scales)
-        wa_sb = load_fp4_words("wa_sb", wa_words, nc.sync)
+        wa_sb = load_fp4_words("wa_sb", wa_words)
         offs_sb = load_list("offs_sb", offs)
         load_plane(wa_plane, wa_scales[:, 0])
-        wb_sb = load_fp4_words("wb_sb", wb_words, nc.sync)
+        wb_sb = load_fp4_words("wb_sb", wb_words)
         load_plane(wb_plane, wb_scales[:, 0])
-        w_sb = load_fp4_words("w_sb", w_words, nc.sync)
+        w_sb = load_fp4_words("w_sb", w_words)
         load_plane(w_plane, w_scales[:, 0])
-        gate2_sb = [keep.tile([P, hi - lo], F32, name="gate2_sb%d" % lo) for lo, hi in pieces(SCATTER_CUTS)]
-        nc.sync.dma_start(gate2_sb[0][:], gate2[:, 0 : SCATTER_CUTS[1]])
+        scatter_parts = pieces((0, SCATTER_CUT, A))
+        gate2_sb = [keep.tile([P, hi - lo], F32, name="gate2_sb%d" % lo) for lo, hi in scatter_parts]
+        nc.sync.dma_start(gate2_sb[0][:], gate2[:, 0:SCATTER_CUT])
         pos_sb = [load_list("pos1_sb", pos1), load_list("pos2_sb", pos2), load_list("pos3_sb", pos3)]
         gate_sb = keep.tile([P, TOP, T], F32, name="gate_sb")
         nc.sync.dma_start(gate_sb[:], gate.rearrange("r p t -> p r t"))
-        nc.sync.dma_start(gate2_sb[1][:], gate2[:, SCATTER_CUTS[1] : A])
+        nc.sync.dma_start(gate2_sb[1][:], gate2[:, SCATTER_CUT:A])
 
         word_window = token_words[:].bitcast(U32)
 
@@ -122,9 +123,10 @@ def tile_moe_mlr_silu_kernel(
                 rhs=wa_codes, rhs_scale=wa_bytes, start=True, stop=True,
             )
             nc.scalar.activation(act[b][:], pre[b][:].rearrange("m (q u v) -> m u q v", u=2, v=2), SILU)
+        turned_banks = (4, 5, 6, 5)
         for b in blocks:
             pairs = act[b][:].rearrange("m u q v -> m (u q v)").bitcast(F32)
-            turned = bank((4, 5, 6, 5)[b], "turned", [P, 2, P])
+            turned = bank(turned_banks[b], "turned", [P, 2, P])
             for u in range(2):
                 nc.tensor.transpose(turned[:, u, :], pairs[:, u * P : (u + 1) * P], identity[:])
             nc.scalar.copy(
@@ -132,12 +134,11 @@ def tile_moe_mlr_silu_kernel(
                 turned[:].rearrange("q u m -> q m u"),
             )
 
-        half = 3 * C
         e_words = keep.tile([P, S], U32, name="e_words", align_bytes=64)
         h_codes = [keep.tile([P, D], U32, name="h_codes", tag="h_codes%d" % f, align_bytes=64) for f in range(F)]
         h_plane = keep.tile([P, A], U8, name="h_plane", align_bytes=64)
         z_sb = keep.tile([P, A], F32, name="z_sb")
-        placed = keep.tile([P, T], F32, name="placed")
+        placed = keep.tile([P, SCATTER_WINDOW], F32, name="placed")
 
         def quantise(f):
             nc.vector.quantize_mx(
@@ -145,10 +146,10 @@ def tile_moe_mlr_silu_kernel(
                 in_=h_grouped[f][:].rearrange("q m t -> q (m t)"),
             )
 
-        def adapter(f):
+        def adapter(f, number):
             slots = slice(f * D, (f + 1) * D)
             wb_codes, wb_bytes = fp4_matrix(wb_sb, wb_plane, f, N)
-            z_bank = bank((4, 7)[f], "z_bank", [P, D])
+            z_bank = bank(number, "z_bank", [P, D])
             nc.tensor.matmul_mx(
                 out=z_bank[:], lhsT=wb_codes, lhsT_scale=wb_bytes,
                 rhs=h_codes[f][:].bitcast(FP8X4), rhs_scale=h_plane[:, slots], start=True, stop=True,
@@ -156,45 +157,46 @@ def tile_moe_mlr_silu_kernel(
             nc.scalar.copy(z_sb[:, slots], z_bank[:])
 
         def scatter(part):
-            lo, hi = pieces(SCATTER_CUTS)[part]
+            lo, hi = scatter_parts[part]
             nc.vector.tensor_tensor(placed[:].indirect(entries(offs2_sb, lo, hi)), z_sb[:, lo:hi], gate2_sb[part][:], MULT)
 
         nc.vector.tensor_copy(e_words[:], word_window.indirect(offs_sb[:]))
-        first_plane = keep.tile([P, half], U8, name="first_plane", align_bytes=64)
-        nc.vector.tensor_copy(first_plane[:], token_plane[:].indirect(entries(offs_sb, 0, half)))
+        first_plane = keep.tile([P, PLANE_CUT], U8, name="first_plane", align_bytes=64)
+        nc.vector.tensor_copy(first_plane[:], token_plane[:].indirect(entries(offs_sb, 0, PLANE_CUT)))
         quantise(0)
-        second_plane = keep.tile([P, S - half], U8, name="second_plane", tag="act3", align_bytes=64)
-        for lo, hi in pieces((half, S - C, S)):
-            nc.vector.tensor_copy(second_plane[:, lo - half : hi - half], token_plane[:].indirect(entries(offs_sb, lo, hi)))
-        adapter(0)
+        second_plane = keep.tile([P, S - PLANE_CUT], U8, name="second_plane", tag="act%d" % blocks[-1], align_bytes=64)
+        for lo, hi in pieces((PLANE_CUT, LAST_EXPERT, S)):
+            nc.vector.tensor_copy(second_plane[:, lo - PLANE_CUT : hi - PLANE_CUT], token_plane[:].indirect(entries(offs_sb, lo, hi)))
+        adapter(0, turned_banks[0])
 
         y_sb = keep.tile([P, S], F32, name="y_sb")
 
-        def experts(lo, hi, number):
-            plane, base = (first_plane, 0) if lo < half else (second_plane, half)
-            y_bank = bank(number, "y_bank", [P, hi - lo])
-            for start, end in pieces([lo] + list(range(lo // C * C + C, hi, C)) + [hi]):
-                w_codes, w_bytes = fp4_matrix(w_sb, w_plane, start // C, N)
+        def experts(first, count, number):
+            plane, base = (first_plane, 0) if first * C < PLANE_CUT else (second_plane, PLANE_CUT)
+            y_bank = bank(number, "y_bank", [P, count * C])
+            for e in range(first, first + count):
+                w_codes, w_bytes = fp4_matrix(w_sb, w_plane, e, N)
                 nc.tensor.matmul_mx(
-                    out=y_bank[:, start - lo : end - lo], lhsT=w_codes, lhsT_scale=w_bytes,
-                    rhs=e_words[:, start:end].bitcast(FP8X4), rhs_scale=plane[:, start - base : end - base],
+                    out=y_bank[:, (e - first) * C : (e - first + 1) * C], lhsT=w_codes, lhsT_scale=w_bytes,
+                    rhs=e_words[:, e * C : (e + 1) * C].bitcast(FP8X4), rhs_scale=plane[:, e * C - base : (e + 1) * C - base],
                     start=True, stop=True,
                 )
-            nc.scalar.copy(y_sb[:, lo:hi], y_bank[:])
+            nc.scalar.copy(y_sb[:, first * C : (first + count) * C], y_bank[:])
 
-        experts(0, C, 6)
-        experts(C, half, 5)
-        experts(half, 4 * C, 0)
-        experts(4 * C, 5 * C, 1)
-        experts(5 * C, S, 7)
+        spare_bank = 7
+        experts(0, 1, turned_banks[2])
+        experts(1, 2, turned_banks[3])
+        experts(3, 1, 0)
+        experts(4, 1, 1)
+        experts(5, 1, spare_bank)
         scatter(0)
         quantise(1)
-        adapter(1)
+        adapter(1, spare_bank)
 
         terms = keep.tile([P, TOP, T], F32, name="terms")
         sums = [bank(b, "sums", [P, N]) for b in range(T // P)]
         sums_sb = keep.tile([P, T // P, N], F32, name="sums_sb")
-        o_banks = [bank(4 + b, "o_bank", [P, P]) for b in range(T // P)]
+        o_banks = [bank(T // P + b, "o_bank", [P, P]) for b in range(T // P)]
 
         def term(r, lo, hi):
             nc.vector.tensor_tensor(

@@ -9,10 +9,9 @@ A = F * D
 P = 128
 PER_COLUMN = 16
 GATHER_WINDOW = 4 * T
-SCATTER_WINDOW = 2 * T
 PLANE_CUT = 3 * C
 LAST_EXPERT = S - C
-SCATTER_CUT = 224
+SCATTER_CUT = D
 FLOPS = 2 * K * N * S + 2 * K * H * A + 2 * H * N * A
 
 F32 = mybir.dt.float32
@@ -138,7 +137,7 @@ def tile_moe_mlr_silu_kernel(
         h_codes = [keep.tile([P, D], U32, name="h_codes", tag="h_codes%d" % f, align_bytes=64) for f in range(F)]
         h_plane = keep.tile([P, A], U8, name="h_plane", align_bytes=64)
         z_sb = keep.tile([P, A], F32, name="z_sb")
-        placed = keep.tile([P, SCATTER_WINDOW], F32, name="placed")
+        placed = keep.tile([P, T], F32, name="placed")
 
         def quantise(f):
             nc.vector.quantize_mx(
@@ -197,29 +196,45 @@ def tile_moe_mlr_silu_kernel(
         sums = [bank(b, "sums", [P, N]) for b in range(T // P)]
         sums_sb = keep.tile([P, T // P, N], F32, name="sums_sb")
         o_banks = [bank(T // P + b, "o_bank", [P, P]) for b in range(T // P)]
+        last = T // P - 1
+        late = slice(last * P, T)
 
-        def term(r, lo, hi):
+        def term(r, hi):
             nc.vector.tensor_tensor(
-                terms[:, r, lo:hi], y_sb[:].indirect(entries(pos_sb[r], lo, hi)), gate_sb[:, r, lo:hi], MULT
+                terms[:, r, 0:hi], y_sb[:].indirect(entries(pos_sb[r], 0, hi)), gate_sb[:, r, 0:hi], MULT
             )
-            for b in range(lo // P, hi // P):
+            for b in range(hi // P):
+                closing = TOP - 2 if b == last else TOP - 1
                 nc.tensor.matmul(
                     sums[b][:], terms[:, r, b * P : (b + 1) * P], identity[:],
-                    start=(r == 0), stop=(r == TOP - 1), is_transpose=True,
+                    start=(r == 0), stop=(r == closing), is_transpose=True,
                 )
 
+        def turn_back(b):
+            nc.scalar.copy(sums_sb[:, b, :], sums[b][:])
+            nc.tensor.transpose(o_banks[b][:], sums_sb[:, b, :], identity[:])
+
         for r in range(TOP - 1):
-            term(r, 0, T)
-        for lo, hi in pieces((0, T // 2, T)):
-            term(TOP - 1, lo, hi)
-            for b in range(lo // P, hi // P):
-                nc.scalar.copy(sums_sb[:, b, :], sums[b][:])
-            for b in range(lo // P, hi // P):
-                nc.tensor.transpose(o_banks[b][:], sums_sb[:, b, :], identity[:])
+            term(r, T)
+        turn_back(last)
+        term(TOP - 1, late.start)
+        for b in range(last):
+            turn_back(b)
         scatter(1)
 
+        late_term = keep.tile([P, P], F32, name="late_term")
+        nc.vector.tensor_tensor(
+            late_term[:], y_sb[:].indirect(entries(pos_sb[TOP - 1], late.start, T)), gate_sb[:, TOP - 1, late], MULT
+        )
+
         result = keep.tile([P, T], F32, name="result")
+        partial = keep.tile([P, P], F32, name="partial")
         for b in range(T // P):
             tokens = slice(b * P, (b + 1) * P)
-            nc.vector.tensor_tensor(result[:, tokens], o_banks[b][:], placed[:, tokens], ADD)
+            if b == last:
+                nc.vector.tensor_tensor(result[:, tokens], partial[:], late_term[:], ADD)
+            else:
+                nc.vector.tensor_tensor(result[:, tokens], o_banks[b][:], placed[:, tokens], ADD)
             (nc.scalar, nc.sync)[b % 2].dma_start(out[:, tokens], result[:, tokens])
+            if b == 0:
+                nc.vector.tensor_tensor(partial[:], o_banks[last][:], placed[:, late], ADD)

@@ -9,7 +9,8 @@ A = F * D
 P = 128
 PER_COLUMN = 16
 GATHER_WINDOW = 4 * T
-PLANE_CUT = 3 * C
+PLANE_CUT = 3 * C + C // 2
+EARLY_EXPERTS = 1
 LAST_EXPERT = S - C
 SCATTER_CUT = D
 FLOPS = 2 * K * N * S + 2 * K * H * A + 2 * H * N * A
@@ -76,39 +77,49 @@ def tile_moe_mlr_silu_kernel(
         def fp4_matrix(words, plane, index, width):
             return words[:, 2 * index * width : 2 * (index + 1) * width].bitcast(FP4X4), plane[:, index * width : (index + 1) * width]
 
+        token_rows = keep.tile([P, T], U8, name="token_rows", align_bytes=64)
+        nc.sync.dma_start(token_rows[:].bitcast(I32), x_scales[0].bitcast(I32).unsqueeze(1).to_broadcast([16, P // 16, T // 4]))
+        offs_sb = load_list("offs_sb", offs)
         token_words = keep.tile([P, GATHER_WINDOW], I32, name="token_words", align_bytes=64)
-        nc.sync.dma_start(token_words[:, 0:T], x_words[0].rearrange("p t d -> p (t d)").bitcast(I32))
         token_plane = zeroed_plane("token_plane", GATHER_WINDOW, T)
         wa_plane = zeroed_plane("wa_plane", F * H, F * H)
         wb_plane = zeroed_plane("wb_plane", F * N, F * N)
         w_plane = zeroed_plane("w_plane", E * N, E * N)
+        early_plane = zeroed_plane("early_plane", C, C)
+        early_rows = keep.tile([P, C], U8, name="early_rows", align_bytes=64)
+        nc.vector.tensor_copy(early_rows[:], token_rows[:].indirect(entries(offs_sb, 0, C)))
 
         identity = keep.tile([P, P], F32, name="identity")
         make_identity(nc, identity[:])
 
         offs2_sb = load_list("offs2_sb", offs2)
         load_plane(token_plane, x_scales)
-        wa_sb = load_fp4_words("wa_sb", wa_words)
-        offs_sb = load_list("offs_sb", offs)
+        nc.sync.dma_start(token_words[:, 0:T], x_words[0].rearrange("p t d -> p (t d)").bitcast(I32))
         load_plane(wa_plane, wa_scales[:, 0])
-        wb_sb = load_fp4_words("wb_sb", wb_words)
-        load_plane(wb_plane, wb_scales[:, 0])
-        w_sb = load_fp4_words("w_sb", w_words)
+        wa_sb = load_fp4_words("wa_sb", wa_words)
+        w_sb = [load_fp4_words("w_sb0", w_words[0:EARLY_EXPERTS])]
         load_plane(w_plane, w_scales[:, 0])
+        for r in range(4):
+            nc.sync.dma_start(early_plane[r:P:32, :].bitcast(I32), early_rows[8 * r : P : 32, :].bitcast(I32))
+        wb_sb = [load_fp4_words("wb_sb0", wb_words[0:1])]
+        load_plane(wb_plane, wb_scales[:, 0])
+        w_sb.append(load_fp4_words("w_sb1", w_words[EARLY_EXPERTS:E]))
+        wb_sb.append(load_fp4_words("wb_sb1", wb_words[1:2]))
         scatter_parts = pieces((0, SCATTER_CUT, A))
         gate2_sb = [keep.tile([P, hi - lo], F32, name="gate2_sb%d" % lo) for lo, hi in scatter_parts]
         nc.sync.dma_start(gate2_sb[0][:], gate2[:, 0:SCATTER_CUT])
-        pos_sb = [load_list("pos1_sb", pos1), load_list("pos2_sb", pos2), load_list("pos3_sb", pos3)]
         gate_sb = keep.tile([P, TOP, T], F32, name="gate_sb")
-        nc.sync.dma_start(gate_sb[:], gate.rearrange("r p t -> p r t"))
+        nc.sync.dma_start(gate_sb[:, 0, :], gate[0])
+        pos_sb = [load_list("pos1_sb", pos1), load_list("pos2_sb", pos2), load_list("pos3_sb", pos3)]
+        nc.sync.dma_start(gate_sb[:, 1:TOP, :], gate[1:TOP].rearrange("r p t -> p r t"))
         nc.sync.dma_start(gate2_sb[1][:], gate2[:, SCATTER_CUT:A])
 
         word_window = token_words[:].bitcast(U32)
 
         a_words = keep.tile([P, A], U32, name="a_words", align_bytes=64)
         a_plane = keep.tile([P, A], U8, name="a_plane", align_bytes=64)
-        nc.vector.tensor_copy(a_words[:], word_window.indirect(offs2_sb[:]))
         nc.vector.tensor_copy(a_plane[:], token_plane[:].indirect(offs2_sb[:]))
+        nc.vector.tensor_copy(a_words[:], word_window.indirect(offs2_sb[:]))
 
         h_grouped = [keep.tile([P, D, 4], BF16, name="h_grouped", tag="h_grouped%d" % f, align_bytes=64) for f in range(F)]
         blocks = range(A // P)
@@ -147,7 +158,7 @@ def tile_moe_mlr_silu_kernel(
 
         def adapter(f, number):
             slots = slice(f * D, (f + 1) * D)
-            wb_codes, wb_bytes = fp4_matrix(wb_sb, wb_plane, f, N)
+            wb_codes, wb_bytes = fp4_matrix(wb_sb[f], wb_plane[:, f * N :], 0, N)
             z_bank = bank(number, "z_bank", [P, D])
             nc.tensor.matmul_mx(
                 out=z_bank[:], lhsT=wb_codes, lhsT_scale=wb_bytes,
@@ -160,8 +171,8 @@ def tile_moe_mlr_silu_kernel(
             nc.vector.tensor_tensor(placed[:].indirect(entries(offs2_sb, lo, hi)), z_sb[:, lo:hi], gate2_sb[part][:], MULT)
 
         nc.vector.tensor_copy(e_words[:], word_window.indirect(offs_sb[:]))
-        first_plane = keep.tile([P, PLANE_CUT], U8, name="first_plane", align_bytes=64)
-        nc.vector.tensor_copy(first_plane[:], token_plane[:].indirect(entries(offs_sb, 0, PLANE_CUT)))
+        first_plane = keep.tile([P, PLANE_CUT - C], U8, name="first_plane", tag="a_plane", align_bytes=64)
+        nc.vector.tensor_copy(first_plane[:], token_plane[:].indirect(entries(offs_sb, C, PLANE_CUT)))
         quantise(0)
         second_plane = keep.tile([P, S - PLANE_CUT], U8, name="second_plane", tag="act%d" % blocks[-1], align_bytes=64)
         for lo, hi in pieces((PLANE_CUT, LAST_EXPERT, S)):
@@ -170,24 +181,28 @@ def tile_moe_mlr_silu_kernel(
 
         y_sb = keep.tile([P, S], F32, name="y_sb")
 
-        def experts(first, count, number):
-            plane, base = (first_plane, 0) if first * C < PLANE_CUT else (second_plane, PLANE_CUT)
-            y_bank = bank(number, "y_bank", [P, count * C])
-            for e in range(first, first + count):
-                w_codes, w_bytes = fp4_matrix(w_sb, w_plane, e, N)
+        def experts(cuts, number):
+            first = cuts[0]
+            plane, base = (early_plane, 0) if first < C else (first_plane, C) if first < PLANE_CUT else (second_plane, PLANE_CUT)
+            y_bank = bank(number, "y_bank", [P, cuts[-1] - first])
+            for lo, hi in pieces(cuts):
+                e = lo // C
+                part = int(e >= EARLY_EXPERTS)
+                w_codes, w_bytes = fp4_matrix(w_sb[part], w_plane[:, part * EARLY_EXPERTS * N :], e - part * EARLY_EXPERTS, N)
                 nc.tensor.matmul_mx(
-                    out=y_bank[:, (e - first) * C : (e - first + 1) * C], lhsT=w_codes, lhsT_scale=w_bytes,
-                    rhs=e_words[:, e * C : (e + 1) * C].bitcast(FP8X4), rhs_scale=plane[:, e * C - base : (e + 1) * C - base],
+                    out=y_bank[:, lo - first : hi - first], lhsT=w_codes, lhsT_scale=w_bytes,
+                    rhs=e_words[:, lo:hi].bitcast(FP8X4), rhs_scale=plane[:, lo - base : hi - base],
                     start=True, stop=True,
                 )
-            nc.scalar.copy(y_sb[:, first * C : (first + count) * C], y_bank[:])
+            nc.scalar.copy(y_sb[:, first : cuts[-1]], y_bank[:])
 
         spare_bank = 7
-        experts(0, 1, turned_banks[2])
-        experts(1, 2, turned_banks[3])
-        experts(3, 1, 0)
-        experts(4, 1, 1)
-        experts(5, 1, spare_bank)
+        experts((0, C), turned_banks[2])
+        experts((C, 2 * C), turned_banks[3])
+        experts((2 * C, 3 * C, PLANE_CUT), 1)
+        experts((PLANE_CUT, 4 * C), 2)
+        experts((4 * C, 5 * C), 0)
+        experts((5 * C, S), spare_bank)
         scatter(0)
         quantise(1)
         adapter(1, spare_bank)

@@ -9,8 +9,8 @@ A = F * D
 P = 128
 PER_COLUMN = 16
 GATHER_WINDOW = 4 * T
-PLANE_CUT = 3 * C + C // 2
-EARLY_EXPERTS = 1
+PLANE_CUT = 3 * C
+HALF_OF_W = E // 2
 LAST_EXPERT = S - C
 SCATTER_CUT = D
 FLOPS = 2 * K * N * S + 2 * K * H * A + 2 * H * N * A
@@ -78,32 +78,31 @@ def tile_moe_mlr_silu_kernel(
             return words[:, 2 * index * width : 2 * (index + 1) * width].bitcast(FP4X4), plane[:, index * width : (index + 1) * width]
 
         token_rows = keep.tile([P, T], U8, name="token_rows", align_bytes=64)
-        nc.sync.dma_start(token_rows[:].bitcast(I32), x_scales[0].bitcast(I32).unsqueeze(1).to_broadcast([16, P // 16, T // 4]))
-        offs_sb = load_list("offs_sb", offs)
+        nc.sync.dma_start(token_rows[:, 0:T].bitcast(I32), x_scales[0].bitcast(I32).unsqueeze(1).to_broadcast([16, P // 16, T // 4]))
+        offs2_sb = load_list("offs2_sb", offs2)
         token_words = keep.tile([P, GATHER_WINDOW], I32, name="token_words", align_bytes=64)
+        nc.sync.dma_start(token_words[:, 0:T], x_words[0].rearrange("p t d -> p (t d)").bitcast(I32))
         token_plane = zeroed_plane("token_plane", GATHER_WINDOW, T)
         wa_plane = zeroed_plane("wa_plane", F * H, F * H)
         wb_plane = zeroed_plane("wb_plane", F * N, F * N)
         w_plane = zeroed_plane("w_plane", E * N, E * N)
-        early_plane = zeroed_plane("early_plane", C, C)
-        early_rows = keep.tile([P, C], U8, name="early_rows", align_bytes=64)
-        nc.vector.tensor_copy(early_rows[:], token_rows[:].indirect(entries(offs_sb, 0, C)))
+        a_planes = [keep.tile([P, D], U8, name="a_plane0", align_bytes=64), zeroed_plane("a_plane1", D, D)]
+        a_rows = keep.tile([P, D], U8, name="a_rows", align_bytes=64)
+        nc.vector.tensor_copy(a_rows[:], token_rows[:].indirect(entries(offs2_sb, D, A)))
 
         identity = keep.tile([P, P], F32, name="identity")
         make_identity(nc, identity[:])
 
-        offs2_sb = load_list("offs2_sb", offs2)
         load_plane(token_plane, x_scales)
-        nc.sync.dma_start(token_words[:, 0:T], x_words[0].rearrange("p t d -> p (t d)").bitcast(I32))
-        load_plane(wa_plane, wa_scales[:, 0])
         wa_sb = load_fp4_words("wa_sb", wa_words)
-        w_sb = [load_fp4_words("w_sb0", w_words[0:EARLY_EXPERTS])]
-        load_plane(w_plane, w_scales[:, 0])
+        offs_sb = load_list("offs_sb", offs)
+        load_plane(wa_plane, wa_scales[:, 0])
         for r in range(4):
-            nc.sync.dma_start(early_plane[r:P:32, :].bitcast(I32), early_rows[8 * r : P : 32, :].bitcast(I32))
+            nc.sync.dma_start(a_planes[1][r:P:32, :].bitcast(I32), a_rows[8 * r : P : 32, :].bitcast(I32))
+        load_plane(w_plane, w_scales[:, 0])
         wb_sb = [load_fp4_words("wb_sb0", wb_words[0:1])]
         load_plane(wb_plane, wb_scales[:, 0])
-        w_sb.append(load_fp4_words("w_sb1", w_words[EARLY_EXPERTS:E]))
+        w_sb = [load_fp4_words("w_sb0", w_words[0:HALF_OF_W]), load_fp4_words("w_sb1", w_words[HALF_OF_W:E])]
         wb_sb.append(load_fp4_words("wb_sb1", wb_words[1:2]))
         scatter_parts = pieces((0, SCATTER_CUT, A))
         gate2_sb = [keep.tile([P, hi - lo], F32, name="gate2_sb%d" % lo) for lo, hi in scatter_parts]
@@ -117,9 +116,8 @@ def tile_moe_mlr_silu_kernel(
         word_window = token_words[:].bitcast(U32)
 
         a_words = keep.tile([P, A], U32, name="a_words", align_bytes=64)
-        a_plane = keep.tile([P, A], U8, name="a_plane", align_bytes=64)
-        nc.vector.tensor_copy(a_plane[:], token_plane[:].indirect(offs2_sb[:]))
         nc.vector.tensor_copy(a_words[:], word_window.indirect(offs2_sb[:]))
+        nc.vector.tensor_copy(a_planes[0][:], token_plane[:].indirect(entries(offs2_sb, 0, D)))
 
         h_grouped = [keep.tile([P, D, 4], BF16, name="h_grouped", tag="h_grouped%d" % f, align_bytes=64) for f in range(F)]
         blocks = range(A // P)
@@ -129,7 +127,7 @@ def tile_moe_mlr_silu_kernel(
             slots = slice(b * P, (b + 1) * P)
             wa_codes, wa_bytes = fp4_matrix(wa_sb, wa_plane, b * P // D, H)
             nc.tensor.matmul_mx(
-                out=pre[b][:], lhsT=a_words[:, slots].bitcast(FP8X4), lhsT_scale=a_plane[:, slots],
+                out=pre[b][:], lhsT=a_words[:, slots].bitcast(FP8X4), lhsT_scale=a_planes[b * P // D][:, b * P % D : b * P % D + P],
                 rhs=wa_codes, rhs_scale=wa_bytes, start=True, stop=True,
             )
             nc.scalar.activation(act[b][:], pre[b][:].rearrange("m (q u v) -> m u q v", u=2, v=2), SILU)
@@ -171,8 +169,8 @@ def tile_moe_mlr_silu_kernel(
             nc.vector.tensor_tensor(placed[:].indirect(entries(offs2_sb, lo, hi)), z_sb[:, lo:hi], gate2_sb[part][:], MULT)
 
         nc.vector.tensor_copy(e_words[:], word_window.indirect(offs_sb[:]))
-        first_plane = keep.tile([P, PLANE_CUT - C], U8, name="first_plane", tag="a_plane", align_bytes=64)
-        nc.vector.tensor_copy(first_plane[:], token_plane[:].indirect(entries(offs_sb, C, PLANE_CUT)))
+        first_plane = keep.tile([P, PLANE_CUT], U8, name="first_plane", align_bytes=64)
+        nc.vector.tensor_copy(first_plane[:], token_plane[:].indirect(entries(offs_sb, 0, PLANE_CUT)))
         quantise(0)
         second_plane = keep.tile([P, S - PLANE_CUT], U8, name="second_plane", tag="act%d" % blocks[-1], align_bytes=64)
         for lo, hi in pieces((PLANE_CUT, LAST_EXPERT, S)):
@@ -183,12 +181,12 @@ def tile_moe_mlr_silu_kernel(
 
         def experts(cuts, number):
             first = cuts[0]
-            plane, base = (early_plane, 0) if first < C else (first_plane, C) if first < PLANE_CUT else (second_plane, PLANE_CUT)
+            plane, base = (first_plane, 0) if first < PLANE_CUT else (second_plane, PLANE_CUT)
             y_bank = bank(number, "y_bank", [P, cuts[-1] - first])
             for lo, hi in pieces(cuts):
                 e = lo // C
-                part = int(e >= EARLY_EXPERTS)
-                w_codes, w_bytes = fp4_matrix(w_sb[part], w_plane[:, part * EARLY_EXPERTS * N :], e - part * EARLY_EXPERTS, N)
+                part = int(e >= HALF_OF_W)
+                w_codes, w_bytes = fp4_matrix(w_sb[part], w_plane[:, part * HALF_OF_W * N :], e - part * HALF_OF_W, N)
                 nc.tensor.matmul_mx(
                     out=y_bank[:, lo - first : hi - first], lhsT=w_codes, lhsT_scale=w_bytes,
                     rhs=e_words[:, lo:hi].bitcast(FP8X4), rhs_scale=plane[:, lo - base : hi - base],
@@ -199,7 +197,7 @@ def tile_moe_mlr_silu_kernel(
         spare_bank = 7
         experts((0, C), turned_banks[2])
         experts((C, 2 * C), turned_banks[3])
-        experts((2 * C, 3 * C, PLANE_CUT), 1)
+        experts((2 * C, PLANE_CUT), 1)
         experts((PLANE_CUT, 4 * C), 2)
         experts((4 * C, 5 * C), 0)
         experts((5 * C, S), spare_bank)

@@ -86,9 +86,9 @@ def tile_moe_mlr_silu_kernel(
         wa_plane = zeroed_plane("wa_plane", F * H, F * H)
         wb_plane = zeroed_plane("wb_plane", F * N, F * N)
         w_plane = zeroed_plane("w_plane", E * N, E * N)
-        a_planes = [keep.tile([P, D], U8, name="a_plane0", align_bytes=64), zeroed_plane("a_plane1", D, D)]
-        a_rows = keep.tile([P, D], U8, name="a_rows", align_bytes=64)
-        nc.vector.tensor_copy(a_rows[:], token_rows[:].indirect(entries(offs2_sb, D, A)))
+        a_planes = [keep.tile([P, P], U8, name="a_plane0", align_bytes=64), zeroed_plane("a_plane1", A - P, A - P)]
+        a_rows = keep.tile([P, A - P], U8, name="a_rows", align_bytes=64)
+        nc.vector.tensor_copy(a_rows[:], token_rows[:].indirect(entries(offs2_sb, P, A)))
 
         identity = keep.tile([P, P], F32, name="identity")
         make_identity(nc, identity[:])
@@ -117,7 +117,7 @@ def tile_moe_mlr_silu_kernel(
 
         a_words = keep.tile([P, A], U32, name="a_words", align_bytes=64)
         nc.vector.tensor_copy(a_words[:], word_window.indirect(offs2_sb[:]))
-        nc.vector.tensor_copy(a_planes[0][:], token_plane[:].indirect(entries(offs2_sb, 0, D)))
+        nc.vector.tensor_copy(a_planes[0][:], token_plane[:, 0:T].indirect(entries(offs2_sb, 0, P)))
 
         h_grouped = [keep.tile([P, D, 4], BF16, name="h_grouped", tag="h_grouped%d" % f, align_bytes=64) for f in range(F)]
         blocks = range(A // P)
@@ -127,7 +127,7 @@ def tile_moe_mlr_silu_kernel(
             slots = slice(b * P, (b + 1) * P)
             wa_codes, wa_bytes = fp4_matrix(wa_sb, wa_plane, b * P // D, H)
             nc.tensor.matmul_mx(
-                out=pre[b][:], lhsT=a_words[:, slots].bitcast(FP8X4), lhsT_scale=a_planes[b * P // D][:, b * P % D : b * P % D + P],
+                out=pre[b][:], lhsT=a_words[:, slots].bitcast(FP8X4), lhsT_scale=a_planes[1][:, (b - 1) * P : b * P] if b else a_planes[0][:],
                 rhs=wa_codes, rhs_scale=wa_bytes, start=True, stop=True,
             )
             nc.scalar.activation(act[b][:], pre[b][:].rearrange("m (q u v) -> m u q v", u=2, v=2), SILU)

@@ -8,11 +8,6 @@ S = E * C
 A = F * D
 P = 128
 PER_COLUMN = 16
-GATHER_WINDOW = 4 * T
-PLANE_CUT = 3 * C
-HALF_OF_W = E // 2
-LAST_EXPERT = S - C
-SCATTER_CUT = D
 FLOPS = 2 * K * N * S + 2 * K * H * A + 2 * H * N * A
 
 F32 = mybir.dt.float32
@@ -26,6 +21,13 @@ FP4X4 = mybir.dt.float4_e2m1fn_x4
 MULT = mybir.AluOpType.mult
 ADD = mybir.AluOpType.add
 SILU = mybir.ActivationFunctionType.Silu
+COPY = mybir.ActivationFunctionType.Copy
+
+GATHER_WINDOW = 4 * T
+WORD_CUTS = (0, 896, S)
+BYTE_CUTS = (0, 512, 1024, 1280, S)
+EARLY_EXPERTS = 2
+ON_SCALAR = 256
 
 
 def pieces(cuts):
@@ -41,31 +43,34 @@ def tile_moe_mlr_silu_kernel(
         keep = ctx.enter_context(tc.tile_pool(name="keep", bufs=1))
         psum = ctx.enter_context(tc.psum_pool(name="psum", bufs=1))
 
+        def sbuf(name, shape, dtype, tag=None):
+            return keep.tile(shape, dtype, name=name, tag=tag or name, align_bytes=64)
+
         def bank(number, name, shape):
             return psum.tile(shape, F32, name=name, tag="bank%d" % number)
 
         def load_list(name, src):
-            offsets = keep.tile([P, src.shape[1]], U16, name=name)
+            offsets = sbuf(name, [P, src.shape[1]], U16)
             nc.sync.dma_start(offsets[:], src)
             return offsets
 
-        def load_fp4_words(name, src):
+        def load_fp4_words(name, src, queue=nc.sync):
             count, width = src.shape[0], src.shape[3]
-            words = keep.tile([P, count * width], U8, name=name, align_bytes=64)
-            nc.sync.dma_start(
+            words = sbuf(name, [P, count * width], U8)
+            queue.dma_start(
                 words[:].bitcast(I32).rearrange("p (e w) -> p e w", e=count),
                 src[:, 0].bitcast(I32).rearrange("e p w -> p e w"),
             )
             return words
 
         def zeroed_plane(name, width, loaded):
-            plane = keep.tile([P, width], U8, name=name, align_bytes=64)
+            plane = sbuf(name, [P, width], U8)
             nc.vector.memset(plane[:, 0:loaded].bitcast(I32), 0)
             return plane
 
-        def load_plane(plane, src):
+        def load_plane(plane, src, rows=range(4)):
             count, width = src.shape[0], src.shape[2]
-            for r in range(4):
+            for r in rows:
                 nc.sync.dma_start(
                     plane[r:P:32, 0 : count * width].bitcast(I32).rearrange("q (e w) -> q e w", e=count),
                     src[:, r:16:4, :].bitcast(I32).rearrange("e q w -> q e w"),
@@ -74,180 +79,189 @@ def tile_moe_mlr_silu_kernel(
         def entries(offsets, lo, hi):
             return offsets[:, lo // PER_COLUMN : hi // PER_COLUMN]
 
-        def fp4_matrix(words, plane, index, width):
-            return words[:, 2 * index * width : 2 * (index + 1) * width].bitcast(FP4X4), plane[:, index * width : (index + 1) * width]
-
-        token_rows = keep.tile([P, T], U8, name="token_rows", align_bytes=64)
-        nc.sync.dma_start(token_rows[:, 0:T].bitcast(I32), x_scales[0].bitcast(I32).unsqueeze(1).to_broadcast([16, P // 16, T // 4]))
+        token_rows = sbuf("token_rows", [P, T], U8)
+        nc.sync.dma_start(token_rows[:].bitcast(I32), x_scales[0].bitcast(I32).unsqueeze(1).to_broadcast([16, P // 16, T // 4]))
         offs2_sb = load_list("offs2_sb", offs2)
-        token_words = keep.tile([P, GATHER_WINDOW], I32, name="token_words", align_bytes=64)
+        token_words = sbuf("token_words", [P, GATHER_WINDOW], I32)
         nc.sync.dma_start(token_words[:, 0:T], x_words[0].rearrange("p t d -> p (t d)").bitcast(I32))
-        token_plane = zeroed_plane("token_plane", GATHER_WINDOW, T)
         wa_plane = zeroed_plane("wa_plane", F * H, F * H)
+        token_plane = zeroed_plane("token_plane", GATHER_WINDOW, T)
         wb_plane = zeroed_plane("wb_plane", F * N, F * N)
         w_plane = zeroed_plane("w_plane", E * N, E * N)
-        a_planes = [keep.tile([P, P], U8, name="a_plane0", align_bytes=64), zeroed_plane("a_plane1", A - P, A - P)]
-        a_rows = keep.tile([P, A - P], U8, name="a_rows", align_bytes=64)
-        nc.vector.tensor_copy(a_rows[:], token_rows[:].indirect(entries(offs2_sb, P, A)))
+        a_planes = [zeroed_plane("a_plane0", A - P, A - P), sbuf("a_plane1", [P, P], U8)]
+        a_rows = sbuf("a_rows", [P, A - P], U8)
+        nc.vector.tensor_copy(a_rows[:], token_rows[:].indirect(entries(offs2_sb, 0, A - P)))
 
-        identity = keep.tile([P, P], F32, name="identity")
+        placed = [sbuf("placed_scalar", [P, T], F32), sbuf("placed_vector", [P, T], F32)]
+        nc.vector.memset(placed[1][:], 0.0)
+        nc.scalar.activation(placed[0][:], placed[1][:], SILU)
+        identity = sbuf("identity", [P, P], F32, "token_rows")
         make_identity(nc, identity[:])
 
-        load_plane(token_plane, x_scales)
+        load_plane(wa_plane, wa_scales[:, 0])
         wa_sb = load_fp4_words("wa_sb", wa_words)
         offs_sb = load_list("offs_sb", offs)
-        load_plane(wa_plane, wa_scales[:, 0])
-        for r in range(4):
-            nc.sync.dma_start(a_planes[1][r:P:32, :].bitcast(I32), a_rows[8 * r : P : 32, :].bitcast(I32))
-        load_plane(w_plane, w_scales[:, 0])
         wb_sb = [load_fp4_words("wb_sb0", wb_words[0:1])]
-        load_plane(wb_plane, wb_scales[:, 0])
-        w_sb = [load_fp4_words("w_sb0", w_words[0:HALF_OF_W]), load_fp4_words("w_sb1", w_words[HALF_OF_W:E])]
-        wb_sb.append(load_fp4_words("wb_sb1", wb_words[1:2]))
-        scatter_parts = pieces((0, SCATTER_CUT, A))
-        gate2_sb = [keep.tile([P, hi - lo], F32, name="gate2_sb%d" % lo) for lo, hi in scatter_parts]
-        nc.sync.dma_start(gate2_sb[0][:], gate2[:, 0:SCATTER_CUT])
-        gate_sb = keep.tile([P, TOP, T], F32, name="gate_sb")
+        for r in range(4):
+            nc.sync.dma_start(a_planes[0][r:P:32, :].bitcast(I32), a_rows[8 * r : P : 32, :].bitcast(I32))
+        load_plane(token_plane, x_scales)
+        gate2_column = sbuf("gate2_column", [P, D // P], F32)
+        with nc.allow_non_contiguous_dma(reason="one weight a partition"):
+            nc.gpsimd.dma_start(gate2_column[:], gate2[0, 0:D].rearrange("(b p) -> p b", p=P))
+        w_sb = [load_fp4_words("w_sb0", w_words[0:EARLY_EXPERTS], nc.gpsimd)]
+        for r in range(4):
+            load_plane(wb_plane, wb_scales[:, 0], [r])
+            load_plane(w_plane, w_scales[:, 0], [r])
+        gate2_sb = sbuf("gate2_sb", [P, D], F32)
+        nc.sync.dma_start(gate2_sb[:], gate2[:, D:A])
+        gate_sb = sbuf("gate_sb", [P, TOP, T], F32)
         nc.sync.dma_start(gate_sb[:, 0, :], gate[0])
-        pos_sb = [load_list("pos1_sb", pos1), load_list("pos2_sb", pos2), load_list("pos3_sb", pos3)]
+        wb_sb.append(load_fp4_words("wb_sb1", wb_words[1:2]))
+        w_sb.append(load_fp4_words("w_sb1", w_words[EARLY_EXPERTS : EARLY_EXPERTS + 2]))
         nc.sync.dma_start(gate_sb[:, 1:TOP, :], gate[1:TOP].rearrange("r p t -> p r t"))
-        nc.sync.dma_start(gate2_sb[1][:], gate2[:, SCATTER_CUT:A])
+        w_sb.append(load_fp4_words("w_sb2", w_words[EARLY_EXPERTS + 2 : E]))
+        pos_sb = [load_list("pos1_sb", pos1), load_list("pos2_sb", pos2), load_list("pos3_sb", pos3)]
 
         word_window = token_words[:].bitcast(U32)
-
-        a_words = keep.tile([P, A], U32, name="a_words", align_bytes=64)
+        a_words = sbuf("a_words", [P, A], U32)
         nc.vector.tensor_copy(a_words[:], word_window.indirect(offs2_sb[:]))
-        nc.vector.tensor_copy(a_planes[0][:], token_plane[:, 0:T].indirect(entries(offs2_sb, 0, P)))
+        nc.vector.tensor_copy(a_planes[1][:], token_plane[:, 0:T].indirect(entries(offs2_sb, A - P, A)))
 
-        h_grouped = [keep.tile([P, D, 4], BF16, name="h_grouped", tag="h_grouped%d" % f, align_bytes=64) for f in range(F)]
-        blocks = range(A // P)
-        pre = [bank(b, "pre", [P, H]) for b in blocks]
-        act = [keep.tile([P, 2, P, 2], BF16, name="act", tag="act%d" % b, align_bytes=64) for b in blocks]
-        for b in blocks:
-            slots = slice(b * P, (b + 1) * P)
-            wa_codes, wa_bytes = fp4_matrix(wa_sb, wa_plane, b * P // D, H)
-            nc.tensor.matmul_mx(
-                out=pre[b][:], lhsT=a_words[:, slots].bitcast(FP8X4), lhsT_scale=a_planes[1][:, (b - 1) * P : b * P] if b else a_planes[0][:],
-                rhs=wa_codes, rhs_scale=wa_bytes, start=True, stop=True,
-            )
-            nc.scalar.activation(act[b][:], pre[b][:].rearrange("m (q u v) -> m u q v", u=2, v=2), SILU)
-        turned_banks = (4, 5, 6, 5)
-        for b in blocks:
-            pairs = act[b][:].rearrange("m u q v -> m (u q v)").bitcast(F32)
-            turned = bank(turned_banks[b], "turned", [P, 2, P])
-            for u in range(2):
-                nc.tensor.transpose(turned[:, u, :], pairs[:, u * P : (u + 1) * P], identity[:])
+        wa_dealt = [sbuf("wa_dealt%d" % f, [P, 2 * H], U8) for f in range(F)]
+        wa_plane_dealt = [sbuf("wa_plane_dealt%d" % f, [P, H], U8) for f in range(F)]
+        for f in range(F):
             nc.scalar.copy(
-                h_grouped[b * P // D][:, b * P % D : b * P % D + P, :].rearrange("q m t -> q (m t)").bitcast(F32).rearrange("q (m u) -> q m u", u=2),
-                turned[:].rearrange("q u m -> q m u"),
+                wa_dealt[f][:].bitcast(U16).rearrange("p (t q) -> p t q", t=4),
+                wa_sb[:, 2 * f * H : 2 * (f + 1) * H].bitcast(U16).rearrange("p (q t) -> p t q", t=4),
+            )
+            nc.gpsimd.tensor_copy(
+                wa_plane_dealt[f][:].rearrange("p (t q) -> p t q", t=4),
+                wa_plane[:, f * H : (f + 1) * H].rearrange("p (q t) -> p t q", t=4),
             )
 
-        e_words = keep.tile([P, S], U32, name="e_words", align_bytes=64)
-        h_codes = [keep.tile([P, D], U32, name="h_codes", tag="h_codes%d" % f, align_bytes=64) for f in range(F)]
-        h_plane = keep.tile([P, A], U8, name="h_plane", align_bytes=64)
-        z_sb = keep.tile([P, A], F32, name="z_sb")
-        placed = keep.tile([P, T], F32, name="placed")
+        h_grouped = [sbuf("h_grouped%d" % f, [P, D, 4], BF16) for f in range(F)]
+        for b in range(A // P):
+            f = b * P // D
+            pre = bank(b, "pre", [P, 4, P])
+            for t in range(4):
+                nc.tensor.matmul_mx(
+                    out=pre[:, t, :],
+                    lhsT=wa_dealt[f][:, 2 * t * P : 2 * (t + 1) * P].bitcast(FP4X4), lhsT_scale=wa_plane_dealt[f][:, t * P : (t + 1) * P],
+                    rhs=a_words[:, b * P : (b + 1) * P].bitcast(FP8X4),
+                    rhs_scale=a_planes[0][:, b * P : (b + 1) * P] if (b + 1) * P < A else a_planes[1][:],
+                    start=True, stop=True,
+                )
+            nc.scalar.activation(h_grouped[f][:, b * P % D : b * P % D + P, :], pre[:].rearrange("q t m -> q m t"), SILU)
 
-        def quantise(f):
+        h_codes = []
+        h_plane = sbuf("h_plane", [P, A], U8)
+        z_sb = sbuf("z_sb", [P, D], F32)
+        gated_turned = sbuf("gated_turned", [P, D // P, N], F32)
+        gated = sbuf("gated", [P, D], F32)
+
+        def adapter(f, tag):
+            h_codes.append(sbuf("h_codes%d" % f, [P, D], U32, tag))
             nc.vector.quantize_mx(
                 out=h_codes[f][:].bitcast(FP8X4), scales=h_plane[:, f * D : (f + 1) * D],
                 in_=h_grouped[f][:].rearrange("q m t -> q (m t)"),
             )
 
-        def adapter(f, number):
-            slots = slice(f * D, (f + 1) * D)
-            wb_codes, wb_bytes = fp4_matrix(wb_sb[f], wb_plane[:, f * N :], 0, N)
-            z_bank = bank(number, "z_bank", [P, D])
-            nc.tensor.matmul_mx(
-                out=z_bank[:], lhsT=wb_codes, lhsT_scale=wb_bytes,
-                rhs=h_codes[f][:].bitcast(FP8X4), rhs_scale=h_plane[:, slots], start=True, stop=True,
-            )
-            nc.scalar.copy(z_sb[:, slots], z_bank[:])
+        word_parts = pieces(WORD_CUTS)
+        e_words = []
 
-        def scatter(part):
-            lo, hi = scatter_parts[part]
-            nc.vector.tensor_tensor(placed[:].indirect(entries(offs2_sb, lo, hi)), z_sb[:, lo:hi], gate2_sb[part][:], MULT)
+        def gather_words(tag):
+            lo, hi = word_parts[len(e_words)]
+            part = sbuf("e_words%d" % lo, [P, hi - lo], U32, tag)
+            nc.vector.tensor_copy(part[:], word_window.indirect(entries(offs_sb, lo, hi)))
+            e_words.append(part)
 
-        nc.vector.tensor_copy(e_words[:], word_window.indirect(offs_sb[:]))
-        first_plane = keep.tile([P, PLANE_CUT], U8, name="first_plane", align_bytes=64)
-        nc.vector.tensor_copy(first_plane[:], token_plane[:].indirect(entries(offs_sb, 0, PLANE_CUT)))
-        quantise(0)
-        second_plane = keep.tile([P, S - PLANE_CUT], U8, name="second_plane", tag="act%d" % blocks[-1], align_bytes=64)
-        for lo, hi in pieces((PLANE_CUT, LAST_EXPERT, S)):
-            nc.vector.tensor_copy(second_plane[:, lo - PLANE_CUT : hi - PLANE_CUT], token_plane[:].indirect(entries(offs_sb, lo, hi)))
-        adapter(0, turned_banks[0])
+        y_sb = sbuf("y_sb", [P, S], F32)
 
-        y_sb = keep.tile([P, S], F32, name="y_sb")
-
-        def experts(cuts, number):
-            first = cuts[0]
-            plane, base = (first_plane, 0) if first < PLANE_CUT else (second_plane, PLANE_CUT)
-            y_bank = bank(number, "y_bank", [P, cuts[-1] - first])
+        def experts(first_expert, count, plane, base, number):
+            y_bank = bank(number, "y_bank", [P, count * C])
+            start, end = first_expert * C, (first_expert + count) * C
+            cuts = sorted(set(range(start, end + 1, C)) | set(c for c in WORD_CUTS if start < c < end))
             for lo, hi in pieces(cuts):
                 e = lo // C
-                part = int(e >= HALF_OF_W)
-                w_codes, w_bytes = fp4_matrix(w_sb[part], w_plane[:, part * HALF_OF_W * N :], e - part * HALF_OF_W, N)
+                part = [n for n, (a, b) in enumerate(word_parts) if a <= lo < b][0]
+                first = word_parts[part][0]
                 nc.tensor.matmul_mx(
-                    out=y_bank[:, lo - first : hi - first], lhsT=w_codes, lhsT_scale=w_bytes,
-                    rhs=e_words[:, lo:hi].bitcast(FP8X4), rhs_scale=plane[:, lo - base : hi - base],
+                    out=y_bank[:, lo - start : hi - start],
+                    lhsT=w_sb[e // 2][:, 2 * (e % 2) * N : 2 * (e % 2 + 1) * N].bitcast(FP4X4), lhsT_scale=w_plane[:, e * N : (e + 1) * N],
+                    rhs=e_words[part][:, lo - first : hi - first].bitcast(FP8X4), rhs_scale=plane[:, lo - base : hi - base],
                     start=True, stop=True,
                 )
-            nc.scalar.copy(y_sb[:, first : cuts[-1]], y_bank[:])
+            nc.scalar.copy(y_sb[:, start:end], y_bank[:])
 
-        spare_bank = 7
-        experts((0, C), turned_banks[2])
-        experts((C, 2 * C), turned_banks[3])
-        experts((2 * C, PLANE_CUT), 1)
-        experts((PLANE_CUT, 4 * C), 2)
-        experts((4 * C, 5 * C), 0)
-        experts((5 * C, S), spare_bank)
-        scatter(0)
-        quantise(1)
-        adapter(1, spare_bank)
-
-        terms = keep.tile([P, TOP, T], F32, name="terms")
-        sums = [bank(b, "sums", [P, N]) for b in range(T // P)]
-        sums_sb = keep.tile([P, T // P, N], F32, name="sums_sb")
-        o_banks = [bank(T // P + b, "o_bank", [P, P]) for b in range(T // P)]
-        last = T // P - 1
-        late = slice(last * P, T)
-
-        def term(r, hi):
-            nc.vector.tensor_tensor(
-                terms[:, r, 0:hi], y_sb[:].indirect(entries(pos_sb[r], 0, hi)), gate_sb[:, r, 0:hi], MULT
+        gather_words(None)
+        first_plane = sbuf("first_plane", [P, BYTE_CUTS[1]], U8)
+        nc.vector.tensor_copy(first_plane[:], token_plane[:].indirect(entries(offs_sb, 0, BYTE_CUTS[1])))
+        adapter(0, None)
+        z_turned = bank(4, "z_turned", [P, D // P, N])
+        for b in range(D // P):
+            nc.tensor.matmul_mx(
+                out=z_turned[:, b, :], lhsT=h_codes[0][:, b * P : (b + 1) * P].bitcast(FP8X4), lhsT_scale=h_plane[:, b * P : (b + 1) * P],
+                rhs=wb_sb[0][:].bitcast(FP4X4), rhs_scale=wb_plane[:, 0:N], start=True, stop=True,
             )
-            for b in range(hi // P):
-                closing = TOP - 2 if b == last else TOP - 1
-                nc.tensor.matmul(
-                    sums[b][:], terms[:, r, b * P : (b + 1) * P], identity[:],
-                    start=(r == 0), stop=(r == closing), is_transpose=True,
-                )
-
-        def turn_back(b):
-            nc.scalar.copy(sums_sb[:, b, :], sums[b][:])
-            nc.tensor.transpose(o_banks[b][:], sums_sb[:, b, :], identity[:])
-
-        for r in range(TOP - 1):
-            term(r, T)
-        turn_back(last)
-        term(TOP - 1, late.start)
-        for b in range(last):
-            turn_back(b)
-        scatter(1)
-
-        late_term = keep.tile([P, P], F32, name="late_term")
+        gated_bank = bank(0, "gated_bank", [P, D])
+        for b in range(D // P):
+            nc.scalar.activation(gated_turned[:, b, :], z_turned[:, b, :], COPY, scale=gate2_column[:, b : b + 1])
+        for b in range(D // P):
+            nc.tensor.transpose(gated_bank[:, b * P : (b + 1) * P], gated_turned[:, b, :], identity[:])
+        nc.scalar.copy(gated[:], gated_bank[:])
+        nc.scalar.activation(placed[0][:].indirect(entries(offs2_sb, 0, D)), gated[:], COPY)
+        experts(0, 2, first_plane, 0, 6)
+        gather_words("h_grouped0")
+        adapter(1, "wb_sb0")
+        z_bank = bank(5, "z_bank", [P, D])
+        nc.tensor.matmul_mx(
+            out=z_bank[:], lhsT=wb_sb[1][:].bitcast(FP4X4), lhsT_scale=wb_plane[:, N : 2 * N],
+            rhs=h_codes[1][:].bitcast(FP8X4), rhs_scale=h_plane[:, D:A], start=True, stop=True,
+        )
+        nc.scalar.copy(z_sb[:], z_bank[:])
+        middle_plane = sbuf("middle_plane", [P, BYTE_CUTS[2] - BYTE_CUTS[1]], U8, "h_codes0")
+        nc.vector.tensor_copy(middle_plane[:], token_plane[:].indirect(entries(offs_sb, BYTE_CUTS[1], BYTE_CUTS[2])))
+        experts(2, 2, middle_plane, BYTE_CUTS[1], 7)
+        second_plane = sbuf("second_plane", [P, S - BYTE_CUTS[2]], U8, "gated_turned")
+        for lo, hi in pieces(BYTE_CUTS[2:]):
+            nc.vector.tensor_copy(second_plane[:, lo - BYTE_CUTS[2] : hi - BYTE_CUTS[2]], token_plane[:].indirect(entries(offs_sb, lo, hi)))
+        for e in range(2 * EARLY_EXPERTS, E):
+            experts(e, 1, second_plane, BYTE_CUTS[2], e - 2)
         nc.vector.tensor_tensor(
-            late_term[:], y_sb[:].indirect(entries(pos_sb[TOP - 1], late.start, T)), gate_sb[:, TOP - 1, late], MULT
+            placed[1][:].indirect(entries(offs2_sb, ON_SCALAR, A)), z_sb[:], gate2_sb[:], MULT
         )
 
-        result = keep.tile([P, T], F32, name="result")
-        partial = keep.tile([P, P], F32, name="partial")
+        sums = [bank(2 + half, "sums", [P, 2, N]) for half in range(2)]
+
+        def add_turned(addend, blocks, first, last):
+            for b in blocks:
+                nc.tensor.matmul(
+                    sums[b // 2][:, b % 2, :], addend[:, b * P : (b + 1) * P], identity[:],
+                    start=first and b % 2 == 0, stop=last and b % 2 == 1, is_transpose=True,
+                )
+
+        add_turned(placed[0], range(T // P), True, False)
+        add_turned(placed[1], range(T // P), False, False)
+
+        raw = sbuf("raw", [P, T], F32)
+        terms = sbuf("terms", [P, TOP, T], F32)
+        sums_sb = sbuf("sums_sb", [P, T // P, N], F32)
+        o_banks = [bank(4 + b, "o_bank", [P, P]) for b in range(T // P)]
+        for lo, hi in pieces((0, T // 2, T)):
+            blocks = range(lo // P, hi // P)
+            nc.scalar.activation(raw[:, lo:hi], y_sb[:].indirect(entries(pos_sb[0], lo, hi)), COPY)
+            nc.vector.tensor_tensor(terms[:, 1, lo:hi], y_sb[:].indirect(entries(pos_sb[1], lo, hi)), gate_sb[:, 1, lo:hi], MULT)
+            add_turned(terms[:, 1, :], blocks, False, False)
+            nc.vector.tensor_tensor(terms[:, 0, lo:hi], raw[:, lo:hi], gate_sb[:, 0, lo:hi], MULT)
+            add_turned(terms[:, 0, :], blocks, False, True)
+        for half in range(2):
+            nc.scalar.copy(sums_sb[:, 2 * half : 2 * half + 2, :], sums[half][:])
+            for b in (2 * half, 2 * half + 1):
+                nc.tensor.transpose(o_banks[b][:], sums_sb[:, b, :], identity[:])
+        nc.vector.tensor_tensor(terms[:, 2, :], y_sb[:].indirect(pos_sb[2][:]), gate_sb[:, 2, :], MULT)
+
+        result = sbuf("result", [P, T], F32)
         for b in range(T // P):
             tokens = slice(b * P, (b + 1) * P)
-            if b == last:
-                nc.vector.tensor_tensor(result[:, tokens], partial[:], late_term[:], ADD)
-            else:
-                nc.vector.tensor_tensor(result[:, tokens], o_banks[b][:], placed[:, tokens], ADD)
+            nc.vector.tensor_tensor(result[:, tokens], o_banks[b][:], terms[:, 2, tokens], ADD)
             (nc.scalar, nc.sync)[b % 2].dma_start(out[:, tokens], result[:, tokens])
-            if b == 0:
-                nc.vector.tensor_tensor(partial[:], o_banks[last][:], placed[:, late], ADD)

@@ -1,7 +1,6 @@
 from contextlib import ExitStack
 
 import concourse.mybir as mybir
-from concourse.masks import make_identity
 
 K, T, E, C, F, D, H, N, TOP = 512, 512, 6, 256, 2, 256, 512, 128, 3
 S = E * C
@@ -24,10 +23,10 @@ SILU = mybir.ActivationFunctionType.Silu
 COPY = mybir.ActivationFunctionType.Copy
 
 GATHER_WINDOW = 4 * T
-WORD_CUTS = (0, 896, S)
-BYTE_CUTS = (0, 512, 1024, 1280, S)
-EARLY_EXPERTS = 2
-ON_SCALAR = 256
+WORD_CUTS = (0, 1152, S)
+BYTE_CUTS = (0, 384, 1024, 1280, S)
+Y_CUTS = (0, 384, 896, 1280, S)
+W_CUTS = (0, 2, E)
 
 
 def pieces(cuts):
@@ -92,35 +91,37 @@ def tile_moe_mlr_silu_kernel(
         a_rows = sbuf("a_rows", [P, A - P], U8)
         nc.vector.tensor_copy(a_rows[:], token_rows[:].indirect(entries(offs2_sb, 0, A - P)))
 
-        placed = [sbuf("placed_scalar", [P, T], F32), sbuf("placed_vector", [P, T], F32)]
-        nc.vector.memset(placed[1][:], 0.0)
-        nc.scalar.activation(placed[0][:], placed[1][:], SILU)
+        placed = sbuf("placed", [P, T], F32)
+        zero = sbuf("zero", [P, 1], F32)
+        nc.vector.memset(zero[:], 0.0)
+        zeros = sbuf("zeros", [P, P], F32)
+        nc.scalar.activation(zeros[:], zero[:].to_broadcast([P, P]), SILU)
         identity = sbuf("identity", [P, P], F32, "token_rows")
-        make_identity(nc, identity[:])
+        nc.gpsimd.affine_select(
+            out=identity[:], in_=zeros[:], compare_op=mybir.AluOpType.not_equal, fill=1.0,
+            base=0, pattern=[[-1, P]], channel_multiplier=1,
+        )
 
         load_plane(wa_plane, wa_scales[:, 0])
         wa_sb = load_fp4_words("wa_sb", wa_words)
         offs_sb = load_list("offs_sb", offs)
-        wb_sb = [load_fp4_words("wb_sb0", wb_words[0:1])]
+        load_plane(token_plane, x_scales, range(2))
         for r in range(4):
             nc.sync.dma_start(a_planes[0][r:P:32, :].bitcast(I32), a_rows[8 * r : P : 32, :].bitcast(I32))
-        load_plane(token_plane, x_scales)
-        gate2_column = sbuf("gate2_column", [P, D // P], F32)
-        with nc.allow_non_contiguous_dma(reason="one weight a partition"):
-            nc.gpsimd.dma_start(gate2_column[:], gate2[0, 0:D].rearrange("(b p) -> p b", p=P))
-        w_sb = [load_fp4_words("w_sb0", w_words[0:EARLY_EXPERTS], nc.gpsimd)]
+        load_plane(token_plane, x_scales, range(2, 4))
+        wb_sb = [load_fp4_words("wb_sb%d" % f, wb_words[f : f + 1]) for f in range(F)]
+        w_sb = [load_fp4_words("w_early", w_words[0 : W_CUTS[1]], nc.gpsimd)]
         for r in range(4):
             load_plane(wb_plane, wb_scales[:, 0], [r])
             load_plane(w_plane, w_scales[:, 0], [r])
-        gate2_sb = sbuf("gate2_sb", [P, D], F32)
-        nc.sync.dma_start(gate2_sb[:], gate2[:, D:A])
+        gate2_sb = sbuf("gate2_sb", [P, A], F32)
+        nc.sync.dma_start(gate2_sb[:], gate2)
         gate_sb = sbuf("gate_sb", [P, TOP, T], F32)
         nc.sync.dma_start(gate_sb[:, 0, :], gate[0])
-        wb_sb.append(load_fp4_words("wb_sb1", wb_words[1:2]))
-        w_sb.append(load_fp4_words("w_sb1", w_words[EARLY_EXPERTS : EARLY_EXPERTS + 2]))
+        pos_sb = [load_list("pos1_sb", pos1), load_list("pos2_sb", pos2)]
+        w_sb.append(load_fp4_words("w_late", w_words[W_CUTS[1] : E]))
         nc.sync.dma_start(gate_sb[:, 1:TOP, :], gate[1:TOP].rearrange("r p t -> p r t"))
-        w_sb.append(load_fp4_words("w_sb2", w_words[EARLY_EXPERTS + 2 : E]))
-        pos_sb = [load_list("pos1_sb", pos1), load_list("pos2_sb", pos2), load_list("pos3_sb", pos3)]
+        pos_sb.append(load_list("pos3_sb", pos3))
 
         word_window = token_words[:].bitcast(U32)
         a_words = sbuf("a_words", [P, A], U32)
@@ -155,9 +156,6 @@ def tile_moe_mlr_silu_kernel(
 
         h_codes = []
         h_plane = sbuf("h_plane", [P, A], U8)
-        z_sb = sbuf("z_sb", [P, D], F32)
-        gated_turned = sbuf("gated_turned", [P, D // P, N], F32)
-        gated = sbuf("gated", [P, D], F32)
 
         def adapter(f, tag):
             h_codes.append(sbuf("h_codes%d" % f, [P, D], U32, tag))
@@ -176,89 +174,99 @@ def tile_moe_mlr_silu_kernel(
             e_words.append(part)
 
         y_sb = sbuf("y_sb", [P, S], F32)
+        planes = []
 
-        def experts(first_expert, count, plane, base, number):
-            y_bank = bank(number, "y_bank", [P, count * C])
-            start, end = first_expert * C, (first_expert + count) * C
-            cuts = sorted(set(range(start, end + 1, C)) | set(c for c in WORD_CUTS if start < c < end))
-            for lo, hi in pieces(cuts):
+        def gather_bytes(tile, base):
+            lo, hi = pieces(BYTE_CUTS)[len(planes)]
+            nc.vector.tensor_copy(tile[:, lo - base : hi - base], token_plane[:].indirect(entries(offs_sb, lo, hi)))
+            planes.append((tile, base, lo, hi))
+
+        def experts(piece, number):
+            start, end = pieces(Y_CUTS)[piece]
+            y_bank = bank(number, "y_bank", [P, end - start])
+            inner = set(range(0, S, C)) | set(WORD_CUTS) | set(BYTE_CUTS)
+            for lo, hi in pieces(sorted(set(c for c in inner if start < c < end) | {start, end})):
                 e = lo // C
                 part = [n for n, (a, b) in enumerate(word_parts) if a <= lo < b][0]
                 first = word_parts[part][0]
+                plane, base = [(tile, base) for tile, base, a, b in planes if a <= lo < b][0]
+                words, place = (w_sb[0], e) if e < W_CUTS[1] else (w_sb[1], e - W_CUTS[1])
                 nc.tensor.matmul_mx(
                     out=y_bank[:, lo - start : hi - start],
-                    lhsT=w_sb[e // 2][:, 2 * (e % 2) * N : 2 * (e % 2 + 1) * N].bitcast(FP4X4), lhsT_scale=w_plane[:, e * N : (e + 1) * N],
+                    lhsT=words[:, 2 * place * N : 2 * (place + 1) * N].bitcast(FP4X4), lhsT_scale=w_plane[:, e * N : (e + 1) * N],
                     rhs=e_words[part][:, lo - first : hi - first].bitcast(FP8X4), rhs_scale=plane[:, lo - base : hi - base],
                     start=True, stop=True,
                 )
             nc.scalar.copy(y_sb[:, start:end], y_bank[:])
 
-        gather_words(None)
-        first_plane = sbuf("first_plane", [P, BYTE_CUTS[1]], U8)
-        nc.vector.tensor_copy(first_plane[:], token_plane[:].indirect(entries(offs_sb, 0, BYTE_CUTS[1])))
-        adapter(0, None)
-        z_turned = bank(4, "z_turned", [P, D // P, N])
-        for b in range(D // P):
+        z_sb = []
+
+        def second_layer(f):
+            z_bank = bank(4 + f, "z_bank", [P, D])
             nc.tensor.matmul_mx(
-                out=z_turned[:, b, :], lhsT=h_codes[0][:, b * P : (b + 1) * P].bitcast(FP8X4), lhsT_scale=h_plane[:, b * P : (b + 1) * P],
-                rhs=wb_sb[0][:].bitcast(FP4X4), rhs_scale=wb_plane[:, 0:N], start=True, stop=True,
+                out=z_bank[:], lhsT=wb_sb[f][:].bitcast(FP4X4), lhsT_scale=wb_plane[:, f * N : (f + 1) * N],
+                rhs=h_codes[f][:].bitcast(FP8X4), rhs_scale=h_plane[:, f * D : (f + 1) * D], start=True, stop=True,
             )
-        gated_bank = bank(0, "gated_bank", [P, D])
-        for b in range(D // P):
-            nc.scalar.activation(gated_turned[:, b, :], z_turned[:, b, :], COPY, scale=gate2_column[:, b : b + 1])
-        for b in range(D // P):
-            nc.tensor.transpose(gated_bank[:, b * P : (b + 1) * P], gated_turned[:, b, :], identity[:])
-        nc.scalar.copy(gated[:], gated_bank[:])
-        nc.scalar.activation(placed[0][:].indirect(entries(offs2_sb, 0, D)), gated[:], COPY)
-        experts(0, 2, first_plane, 0, 6)
-        gather_words("h_grouped0")
+            z_sb.append(sbuf("z_sb%d" % f, [P, D], F32))
+            nc.scalar.copy(z_sb[f][:], z_bank[:])
+
+        gather_words(None)
+        gather_bytes(sbuf("first_plane", [P, BYTE_CUTS[1]], U8), 0)
+        adapter(0, None)
+        second_layer(0)
+        gated = sbuf("gated", [P, D], F32)
+        nc.gpsimd.tensor_tensor(gated[:], z_sb[0][:], gate2_sb[:, 0:D], MULT)
+        experts(0, 6)
+        gather_words("a_words")
         adapter(1, "wb_sb0")
-        z_bank = bank(5, "z_bank", [P, D])
-        nc.tensor.matmul_mx(
-            out=z_bank[:], lhsT=wb_sb[1][:].bitcast(FP4X4), lhsT_scale=wb_plane[:, N : 2 * N],
-            rhs=h_codes[1][:].bitcast(FP8X4), rhs_scale=h_plane[:, D:A], start=True, stop=True,
-        )
-        nc.scalar.copy(z_sb[:], z_bank[:])
-        middle_plane = sbuf("middle_plane", [P, BYTE_CUTS[2] - BYTE_CUTS[1]], U8, "h_codes0")
-        nc.vector.tensor_copy(middle_plane[:], token_plane[:].indirect(entries(offs_sb, BYTE_CUTS[1], BYTE_CUTS[2])))
-        experts(2, 2, middle_plane, BYTE_CUTS[1], 7)
-        second_plane = sbuf("second_plane", [P, S - BYTE_CUTS[2]], U8, "gated_turned")
-        for lo, hi in pieces(BYTE_CUTS[2:]):
-            nc.vector.tensor_copy(second_plane[:, lo - BYTE_CUTS[2] : hi - BYTE_CUTS[2]], token_plane[:].indirect(entries(offs_sb, lo, hi)))
-        for e in range(2 * EARLY_EXPERTS, E):
-            experts(e, 1, second_plane, BYTE_CUTS[2], e - 2)
-        nc.vector.tensor_tensor(
-            placed[1][:].indirect(entries(offs2_sb, ON_SCALAR, A)), z_sb[:], gate2_sb[:], MULT
-        )
+        second_layer(1)
+        nc.scalar.activation(placed[:].indirect(entries(offs2_sb, 0, D)), gated[:], COPY)
+        gather_bytes(sbuf("middle_plane", [P, BYTE_CUTS[2] - BYTE_CUTS[1]], U8, "h_codes0"), BYTE_CUTS[1])
+        experts(1, 7)
+        last_plane = sbuf("last_plane", [P, S - BYTE_CUTS[2]], U8, "z_sb0")
+        gather_bytes(last_plane, BYTE_CUTS[2])
+        gather_bytes(last_plane, BYTE_CUTS[2])
+        experts(2, 2)
+        experts(3, 3)
+        nc.vector.tensor_tensor(placed[:].indirect(entries(offs2_sb, D, A)), z_sb[1][:], gate2_sb[:, D:A], MULT)
 
-        sums = [bank(2 + half, "sums", [P, 2, N]) for half in range(2)]
+        groups = ((0, 1), (2,), (3,))
+        sums = [bank(number, "sums", [P, len(group), N]) for number, group in zip((2, 3, 0), groups)]
 
-        def add_turned(addend, blocks, first, last):
-            for b in blocks:
-                nc.tensor.matmul(
-                    sums[b // 2][:, b % 2, :], addend[:, b * P : (b + 1) * P], identity[:],
-                    start=first and b % 2 == 0, stop=last and b % 2 == 1, is_transpose=True,
-                )
+        opened = set()
 
-        add_turned(placed[0], range(T // P), True, False)
-        add_turned(placed[1], range(T // P), False, False)
+        def add_turned(addend, blocks, last):
+            for tile, group in zip(sums, groups):
+                for place, b in enumerate(group):
+                    if b in blocks:
+                        nc.tensor.matmul(
+                            tile[:, place, :], addend[:, b * P : (b + 1) * P], identity[:],
+                            start=group not in opened, stop=last and b == group[-1], is_transpose=True,
+                        )
+                        opened.add(group)
+
+        add_turned(placed, range(3), False)
 
         raw = sbuf("raw", [P, T], F32)
         terms = sbuf("terms", [P, TOP, T], F32)
         sums_sb = sbuf("sums_sb", [P, T // P, N], F32)
         o_banks = [bank(4 + b, "o_bank", [P, P]) for b in range(T // P)]
-        for lo, hi in pieces((0, T // 2, T)):
+        halves = pieces((0, T // 2, T))
+        for lo, hi in halves:
             blocks = range(lo // P, hi // P)
             nc.scalar.activation(raw[:, lo:hi], y_sb[:].indirect(entries(pos_sb[0], lo, hi)), COPY)
             nc.vector.tensor_tensor(terms[:, 1, lo:hi], y_sb[:].indirect(entries(pos_sb[1], lo, hi)), gate_sb[:, 1, lo:hi], MULT)
-            add_turned(terms[:, 1, :], blocks, False, False)
+            add_turned(terms[:, 1, :], blocks, False)
+            if lo:
+                add_turned(placed, [3], False)
             nc.vector.tensor_tensor(terms[:, 0, lo:hi], raw[:, lo:hi], gate_sb[:, 0, lo:hi], MULT)
-            add_turned(terms[:, 0, :], blocks, False, True)
-        for half in range(2):
-            nc.scalar.copy(sums_sb[:, 2 * half : 2 * half + 2, :], sums[half][:])
-            for b in (2 * half, 2 * half + 1):
+            add_turned(terms[:, 0, :], blocks, True)
+        for tile, group in zip(sums, groups):
+            nc.scalar.copy(sums_sb[:, group[0] : group[-1] + 1, :], tile[:])
+            for b in group:
                 nc.tensor.transpose(o_banks[b][:], sums_sb[:, b, :], identity[:])
-        nc.vector.tensor_tensor(terms[:, 2, :], y_sb[:].indirect(pos_sb[2][:]), gate_sb[:, 2, :], MULT)
+        for lo, hi in halves:
+            nc.vector.tensor_tensor(terms[:, 2, lo:hi], y_sb[:].indirect(entries(pos_sb[2], lo, hi)), gate_sb[:, 2, lo:hi], MULT)
 
         result = sbuf("result", [P, T], F32)
         for b in range(T // P):

@@ -91,9 +91,11 @@ def tile_moe_mlr_silu_kernel(
         a_rows = sbuf("a_rows", [P, A - P], U8)
         nc.vector.tensor_copy(a_rows[:], token_rows[:].indirect(entries(offs2_sb, 0, A - P)))
 
-        placed = sbuf("placed", [P, T], F32)
+        placed = [sbuf("placed_scalar", [P, T], F32), sbuf("placed_vector", [P, T], F32)]
         zero = sbuf("zero", [P, 1], F32)
         nc.vector.memset(zero[:], 0.0)
+        for window in placed:
+            nc.scalar.activation(window[:], zero[:].to_broadcast([P, T]), SILU)
         zeros = sbuf("zeros", [P, P], F32)
         nc.scalar.activation(zeros[:], zero[:].to_broadcast([P, P]), SILU)
         identity = sbuf("identity", [P, P], F32, "token_rows")
@@ -114,12 +116,13 @@ def tile_moe_mlr_silu_kernel(
         for r in range(4):
             load_plane(wb_plane, wb_scales[:, 0], [r])
             load_plane(w_plane, w_scales[:, 0], [r])
-        gate2_sb = sbuf("gate2_sb", [P, A], F32)
-        nc.sync.dma_start(gate2_sb[:], gate2)
+        gate2_sb = [sbuf("gate2_sb%d" % f, [P, D], F32) for f in range(F)]
+        nc.sync.dma_start(gate2_sb[0][:], gate2[:, 0:D])
         gate_sb = sbuf("gate_sb", [P, TOP, T], F32)
         nc.sync.dma_start(gate_sb[:, 0, :], gate[0])
         pos_sb = [load_list("pos1_sb", pos1), load_list("pos2_sb", pos2)]
         w_sb.append(load_fp4_words("w_late", w_words[W_CUTS[1] : E]))
+        nc.sync.dma_start(gate2_sb[1][:], gate2[:, D:A])
         nc.sync.dma_start(gate_sb[:, 1:TOP, :], gate[1:TOP].rearrange("r p t -> p r t"))
         pos_sb.append(load_list("pos3_sb", pos3))
 
@@ -215,12 +218,12 @@ def tile_moe_mlr_silu_kernel(
         adapter(0, None)
         second_layer(0)
         gated = sbuf("gated", [P, D], F32)
-        nc.gpsimd.tensor_tensor(gated[:], z_sb[0][:], gate2_sb[:, 0:D], MULT)
+        nc.gpsimd.tensor_tensor(gated[:], z_sb[0][:], gate2_sb[0][:], MULT)
         experts(0, 6)
         gather_words("a_words")
         adapter(1, "wb_sb0")
         second_layer(1)
-        nc.scalar.activation(placed[:].indirect(entries(offs2_sb, 0, D)), gated[:], COPY)
+        nc.scalar.activation(placed[0][:].indirect(entries(offs2_sb, 0, D)), gated[:], COPY)
         gather_bytes(sbuf("middle_plane", [P, BYTE_CUTS[2] - BYTE_CUTS[1]], U8, "h_codes0"), BYTE_CUTS[1])
         experts(1, 7)
         last_plane = sbuf("last_plane", [P, S - BYTE_CUTS[2]], U8, "z_sb0")
@@ -228,7 +231,7 @@ def tile_moe_mlr_silu_kernel(
         gather_bytes(last_plane, BYTE_CUTS[2])
         experts(2, 2)
         experts(3, 3)
-        nc.vector.tensor_tensor(placed[:].indirect(entries(offs2_sb, D, A)), z_sb[1][:], gate2_sb[:, D:A], MULT)
+        nc.vector.tensor_tensor(placed[1][:].indirect(entries(offs2_sb, D, A)), z_sb[1][:], gate2_sb[1][:], MULT)
 
         groups = ((0, 1), (2,), (3,))
         sums = [bank(number, "sums", [P, len(group), N]) for number, group in zip((2, 3, 0), groups)]
@@ -245,7 +248,8 @@ def tile_moe_mlr_silu_kernel(
                         )
                         opened.add(group)
 
-        add_turned(placed, range(3), False)
+        for window in placed:
+            add_turned(window, range(3), False)
 
         raw = sbuf("raw", [P, T], F32)
         terms = sbuf("terms", [P, TOP, T], F32)
@@ -258,7 +262,8 @@ def tile_moe_mlr_silu_kernel(
             nc.vector.tensor_tensor(terms[:, 1, lo:hi], y_sb[:].indirect(entries(pos_sb[1], lo, hi)), gate_sb[:, 1, lo:hi], MULT)
             add_turned(terms[:, 1, :], blocks, False)
             if lo:
-                add_turned(placed, [3], False)
+                for window in placed:
+                    add_turned(window, [3], False)
             nc.vector.tensor_tensor(terms[:, 0, lo:hi], raw[:, lo:hi], gate_sb[:, 0, lo:hi], MULT)
             add_turned(terms[:, 0, :], blocks, True)
         for tile, group in zip(sums, groups):

@@ -24,7 +24,7 @@ COPY = mybir.ActivationFunctionType.Copy
 
 GATHER_WINDOW = 4 * T
 WORD_CUTS = (0, 1152, S)
-BYTE_CUTS = (0, 384, 1024, 1280, S)
+BYTE_CUTS = (0, 384, 1024, 1280, 1408, S)
 Y_CUTS = (0, 384, 896, 1280, S)
 W_CUTS = (0, 2, E)
 
@@ -181,7 +181,8 @@ def tile_moe_mlr_silu_kernel(
 
         def gather_bytes(tile, base):
             lo, hi = pieces(BYTE_CUTS)[len(planes)]
-            nc.vector.tensor_copy(tile[:, lo - base : hi - base], token_plane[:].indirect(entries(offs_sb, lo, hi)))
+            window = token_plane[:] if hi - lo > P else token_plane[:, 0:T]
+            nc.vector.tensor_copy(tile[:, lo - base : hi - base], window.indirect(entries(offs_sb, lo, hi)))
             planes.append((tile, base, lo, hi))
 
         def experts(piece, number):
@@ -227,14 +228,14 @@ def tile_moe_mlr_silu_kernel(
         gather_bytes(sbuf("middle_plane", [P, BYTE_CUTS[2] - BYTE_CUTS[1]], U8, "h_codes0"), BYTE_CUTS[1])
         experts(1, 7)
         last_plane = sbuf("last_plane", [P, S - BYTE_CUTS[2]], U8, "z_sb0")
-        gather_bytes(last_plane, BYTE_CUTS[2])
-        gather_bytes(last_plane, BYTE_CUTS[2])
+        for cut in BYTE_CUTS[3:]:
+            gather_bytes(last_plane, BYTE_CUTS[2])
         experts(2, 2)
         experts(3, 3)
         nc.vector.tensor_tensor(placed[1][:].indirect(entries(offs2_sb, D, A)), z_sb[1][:], gate2_sb[1][:], MULT)
 
         groups = ((0, 1), (2,), (3,))
-        sums = [bank(number, "sums", [P, len(group), N]) for number, group in zip((2, 3, 0), groups)]
+        sums = [bank(number, "sums", [P, len(group), N]) for number, group in zip((2, 3, 7), groups)]
 
         opened = set()
 
@@ -249,21 +250,18 @@ def tile_moe_mlr_silu_kernel(
                         opened.add(group)
 
         for window in placed:
-            add_turned(window, range(3), False)
+            add_turned(window, range(T // P), False)
 
         raw = sbuf("raw", [P, T], F32)
         terms = sbuf("terms", [P, TOP, T], F32)
         sums_sb = sbuf("sums_sb", [P, T // P, N], F32)
-        o_banks = [bank(4 + b, "o_bank", [P, P]) for b in range(T // P)]
+        o_banks = [bank(number, "o_bank", [P, P]) for number in (4, 5, 6, 0)]
         halves = pieces((0, T // 2, T))
         for lo, hi in halves:
             blocks = range(lo // P, hi // P)
             nc.scalar.activation(raw[:, lo:hi], y_sb[:].indirect(entries(pos_sb[0], lo, hi)), COPY)
             nc.vector.tensor_tensor(terms[:, 1, lo:hi], y_sb[:].indirect(entries(pos_sb[1], lo, hi)), gate_sb[:, 1, lo:hi], MULT)
             add_turned(terms[:, 1, :], blocks, False)
-            if lo:
-                for window in placed:
-                    add_turned(window, [3], False)
             nc.vector.tensor_tensor(terms[:, 0, lo:hi], raw[:, lo:hi], gate_sb[:, 0, lo:hi], MULT)
             add_turned(terms[:, 0, :], blocks, True)
         for tile, group in zip(sums, groups):

from contextlib import ExitStack

import concourse.mybir as mybir

K, T, E, C, F, D, H, N, TOP = 512, 512, 6, 256, 2, 256, 512, 128, 3
S = E * C
A = F * D
P = 128
PER_COLUMN = 16
FLOPS = 2 * K * N * S + 2 * K * H * A + 2 * H * N * A

F32 = mybir.dt.float32
BF16 = mybir.dt.bfloat16
I32 = mybir.dt.int32
U32 = mybir.dt.uint32
U16 = mybir.dt.uint16
U8 = mybir.dt.uint8
FP8X4 = mybir.dt.float8_e4m3fn_x4
FP4X4 = mybir.dt.float4_e2m1fn_x4
MULT = mybir.AluOpType.mult
ADD = mybir.AluOpType.add
SILU = mybir.ActivationFunctionType.Silu
COPY = mybir.ActivationFunctionType.Copy

GATHER_WINDOW = 4 * T
WORD_CUTS = (0, 1152, S)
BYTE_CUTS = (0, 384, 1024, 1280, 1408, S)
Y_CUTS = (0, 384, 896, 1280, S)
W_CUTS = (0, 2, E)


def pieces(cuts):
    return list(zip(cuts[:-1], cuts[1:]))


def tile_moe_mlr_silu_kernel(
    tc, x_words, x_scales, w_words, w_scales, wa_words, wa_scales, wb_words, wb_scales,
    gate, gate2, offs, pos1, pos2, pos3, offs2, out,
):
    nc = tc.nc
    with ExitStack() as ctx:
        keep = ctx.enter_context(tc.tile_pool(name="keep", bufs=1))
        psum = ctx.enter_context(tc.psum_pool(name="psum", bufs=1))

        def sbuf(name, shape, dtype, tag=None):
            return keep.tile(shape, dtype, name=name, tag=tag or name, align_bytes=64)

        def bank(number, name, shape):
            return psum.tile(shape, F32, name=name, tag="bank%d" % number)

        def load_list(name, src):
            offsets = sbuf(name, [P, src.shape[1]], U16)
            nc.sync.dma_start(offsets[:], src)
            return offsets

        def load_fp4_words(name, src, queue=nc.sync):
            count, width = src.shape[0], src.shape[3]
            words = sbuf(name, [P, count * width], U8)
            queue.dma_start(
                words[:].bitcast(I32).rearrange("p (e w) -> p e w", e=count),
                src[:, 0].bitcast(I32).rearrange("e p w -> p e w"),
            )
            return words

        def zeroed_plane(name, width, loaded):
            plane = sbuf(name, [P, width], U8)
            nc.vector.memset(plane[:, 0:loaded].bitcast(I32), 0)
            return plane

        def load_plane(plane, src, rows=range(4)):
            count, width = src.shape[0], src.shape[2]
            for r in rows:
                nc.sync.dma_start(
                    plane[r:P:32, 0 : count * width].bitcast(I32).rearrange("q (e w) -> q e w", e=count),
                    src[:, r:16:4, :].bitcast(I32).rearrange("e q w -> q e w"),
                )

        def entries(offsets, lo, hi):
            return offsets[:, lo // PER_COLUMN : hi // PER_COLUMN]

        token_rows = sbuf("token_rows", [P, T], U8)
        nc.sync.dma_start(token_rows[:].bitcast(I32), x_scales[0].bitcast(I32).unsqueeze(1).to_broadcast([16, P // 16, T // 4]))
        offs2_sb = load_list("offs2_sb", offs2)
        token_words = sbuf("token_words", [P, GATHER_WINDOW], I32)
        nc.sync.dma_start(token_words[:, 0:T], x_words[0].rearrange("p t d -> p (t d)").bitcast(I32))
        wa_plane = zeroed_plane("wa_plane", F * H, F * H)
        token_plane = zeroed_plane("token_plane", GATHER_WINDOW, T)
        wb_plane = zeroed_plane("wb_plane", F * N, F * N)
        w_plane = zeroed_plane("w_plane", E * N, E * N)
        a_planes = [zeroed_plane("a_plane0", A - P, A - P), sbuf("a_plane1", [P, P], U8)]
        a_rows = sbuf("a_rows", [P, A - P], U8)
        nc.vector.tensor_copy(a_rows[:], token_rows[:].indirect(entries(offs2_sb, 0, A - P)))

        placed = [sbuf("placed_scalar", [P, T], F32), sbuf("placed_vector", [P, T], F32)]
        zero = sbuf("zero", [P, 1], F32)
        nc.vector.memset(zero[:], 0.0)
        for window in placed:
            nc.scalar.activation(window[:], zero[:].to_broadcast([P, T]), SILU)
        zeros = sbuf("zeros", [P, P], F32)
        nc.scalar.activation(zeros[:], zero[:].to_broadcast([P, P]), SILU)
        identity = sbuf("identity", [P, P], F32, "token_rows")
        nc.gpsimd.affine_select(
            out=identity[:], in_=zeros[:], compare_op=mybir.AluOpType.not_equal, fill=1.0,
            base=0, pattern=[[-1, P]], channel_multiplier=1,
        )

        load_plane(wa_plane, wa_scales[:, 0])
        wa_sb = load_fp4_words("wa_sb", wa_words)
        offs_sb = load_list("offs_sb", offs)
        load_plane(token_plane, x_scales, range(2))
        for r in range(4):
            nc.sync.dma_start(a_planes[0][r:P:32, :].bitcast(I32), a_rows[8 * r : P : 32, :].bitcast(I32))
        load_plane(token_plane, x_scales, range(2, 4))
        wb_sb = [load_fp4_words("wb_sb%d" % f, wb_words[f : f + 1]) for f in range(F)]
        w_sb = [load_fp4_words("w_early", w_words[0 : W_CUTS[1]], nc.gpsimd)]
        for r in range(4):
            load_plane(wb_plane, wb_scales[:, 0], [r])
            load_plane(w_plane, w_scales[:, 0], [r])
        gate2_sb = [sbuf("gate2_sb%d" % f, [P, D], F32) for f in range(F)]
        nc.sync.dma_start(gate2_sb[0][:], gate2[:, 0:D])
        gate_sb = sbuf("gate_sb", [P, TOP, T], F32)
        nc.sync.dma_start(gate_sb[:, 0, :], gate[0])
        pos_sb = [load_list("pos1_sb", pos1), load_list("pos2_sb", pos2)]
        w_sb.append(load_fp4_words("w_late", w_words[W_CUTS[1] : E]))
        nc.sync.dma_start(gate2_sb[1][:], gate2[:, D:A])
        nc.sync.dma_start(gate_sb[:, 1:TOP, :], gate[1:TOP].rearrange("r p t -> p r t"))
        pos_sb.append(load_list("pos3_sb", pos3))

        word_window = token_words[:].bitcast(U32)
        a_words = sbuf("a_words", [P, A], U32)
        nc.vector.tensor_copy(a_words[:], word_window.indirect(offs2_sb[:]))
        nc.vector.tensor_copy(a_planes[1][:], token_plane[:, 0:T].indirect(entries(offs2_sb, A - P, A)))

        wa_dealt = [sbuf("wa_dealt%d" % f, [P, 2 * H], U8) for f in range(F)]
        wa_plane_dealt = [sbuf("wa_plane_dealt%d" % f, [P, H], U8) for f in range(F)]
        for f in range(F):
            nc.scalar.copy(
                wa_dealt[f][:].bitcast(U16).rearrange("p (t q) -> p t q", t=4),
                wa_sb[:, 2 * f * H : 2 * (f + 1) * H].bitcast(U16).rearrange("p (q t) -> p t q", t=4),
            )
            nc.gpsimd.tensor_copy(
                wa_plane_dealt[f][:].rearrange("p (t q) -> p t q", t=4),
                wa_plane[:, f * H : (f + 1) * H].rearrange("p (q t) -> p t q", t=4),
            )

        h_grouped = [sbuf("h_grouped%d" % f, [P, D, 4], BF16) for f in range(F)]
        for b in range(A // P):
            f = b * P // D
            pre = bank(b, "pre", [P, 4, P])
            for t in range(4):
                nc.tensor.matmul_mx(
                    out=pre[:, t, :],
                    lhsT=wa_dealt[f][:, 2 * t * P : 2 * (t + 1) * P].bitcast(FP4X4), lhsT_scale=wa_plane_dealt[f][:, t * P : (t + 1) * P],
                    rhs=a_words[:, b * P : (b + 1) * P].bitcast(FP8X4),
                    rhs_scale=a_planes[0][:, b * P : (b + 1) * P] if (b + 1) * P < A else a_planes[1][:],
                    start=True, stop=True,
                )
            nc.scalar.activation(h_grouped[f][:, b * P % D : b * P % D + P, :], pre[:].rearrange("q t m -> q m t"), SILU)

        h_codes = []
        h_plane = sbuf("h_plane", [P, A], U8)

        def adapter(f, tag):
            h_codes.append(sbuf("h_codes%d" % f, [P, D], U32, tag))
            nc.vector.quantize_mx(
                out=h_codes[f][:].bitcast(FP8X4), scales=h_plane[:, f * D : (f + 1) * D],
                in_=h_grouped[f][:].rearrange("q m t -> q (m t)"),
            )

        word_parts = pieces(WORD_CUTS)
        e_words = []

        def gather_words(tag):
            lo, hi = word_parts[len(e_words)]
            part = sbuf("e_words%d" % lo, [P, hi - lo], U32, tag)
            nc.vector.tensor_copy(part[:], word_window.indirect(entries(offs_sb, lo, hi)))
            e_words.append(part)

        y_sb = sbuf("y_sb", [P, S], F32)
        planes = []

        def gather_bytes(tile, base):
            lo, hi = pieces(BYTE_CUTS)[len(planes)]
            window = token_plane[:] if hi - lo > P else token_plane[:, 0:T]
            nc.vector.tensor_copy(tile[:, lo - base : hi - base], window.indirect(entries(offs_sb, lo, hi)))
            planes.append((tile, base, lo, hi))

        def experts(piece, number):
            start, end = pieces(Y_CUTS)[piece]
            y_bank = bank(number, "y_bank", [P, end - start])
            inner = set(range(0, S, C)) | set(WORD_CUTS) | set(BYTE_CUTS)
            for lo, hi in pieces(sorted(set(c for c in inner if start < c < end) | {start, end})):
                e = lo // C
                part = [n for n, (a, b) in enumerate(word_parts) if a <= lo < b][0]
                first = word_parts[part][0]
                plane, base = [(tile, base) for tile, base, a, b in planes if a <= lo < b][0]
                words, place = (w_sb[0], e) if e < W_CUTS[1] else (w_sb[1], e - W_CUTS[1])
                nc.tensor.matmul_mx(
                    out=y_bank[:, lo - start : hi - start],
                    lhsT=words[:, 2 * place * N : 2 * (place + 1) * N].bitcast(FP4X4), lhsT_scale=w_plane[:, e * N : (e + 1) * N],
                    rhs=e_words[part][:, lo - first : hi - first].bitcast(FP8X4), rhs_scale=plane[:, lo - base : hi - base],
                    start=True, stop=True,
                )
            nc.scalar.copy(y_sb[:, start:end], y_bank[:])

        z_sb = []

        def second_layer(f):
            z_bank = bank(4 + f, "z_bank", [P, D])
            nc.tensor.matmul_mx(
                out=z_bank[:], lhsT=wb_sb[f][:].bitcast(FP4X4), lhsT_scale=wb_plane[:, f * N : (f + 1) * N],
                rhs=h_codes[f][:].bitcast(FP8X4), rhs_scale=h_plane[:, f * D : (f + 1) * D], start=True, stop=True,
            )
            z_sb.append(sbuf("z_sb%d" % f, [P, D], F32))
            nc.scalar.copy(z_sb[f][:], z_bank[:])

        gather_words(None)
        gather_bytes(sbuf("first_plane", [P, BYTE_CUTS[1]], U8), 0)
        adapter(0, None)
        second_layer(0)
        gated = sbuf("gated", [P, D], F32)
        nc.gpsimd.tensor_tensor(gated[:], z_sb[0][:], gate2_sb[0][:], MULT)
        experts(0, 6)
        gather_words("a_words")
        adapter(1, "wb_sb0")
        second_layer(1)
        nc.scalar.activation(placed[0][:].indirect(entries(offs2_sb, 0, D)), gated[:], COPY)
        gather_bytes(sbuf("middle_plane", [P, BYTE_CUTS[2] - BYTE_CUTS[1]], U8, "h_codes0"), BYTE_CUTS[1])
        experts(1, 7)
        last_plane = sbuf("last_plane", [P, S - BYTE_CUTS[2]], U8, "z_sb0")
        for cut in BYTE_CUTS[3:]:
            gather_bytes(last_plane, BYTE_CUTS[2])
        experts(2, 2)
        experts(3, 3)
        nc.vector.tensor_tensor(placed[1][:].indirect(entries(offs2_sb, D, A)), z_sb[1][:], gate2_sb[1][:], MULT)

        groups = ((0, 1), (2,), (3,))
        sums = [bank(number, "sums", [P, len(group), N]) for number, group in zip((2, 3, 7), groups)]

        opened = set()

        def add_turned(addend, blocks, last):
            for tile, group in zip(sums, groups):
                for place, b in enumerate(group):
                    if b in blocks:
                        nc.tensor.matmul(
                            tile[:, place, :], addend[:, b * P : (b + 1) * P], identity[:],
                            start=group not in opened, stop=last and b == group[-1], is_transpose=True,
                        )
                        opened.add(group)

        for window in placed:
            add_turned(window, range(T // P), False)

        raw = sbuf("raw", [P, T], F32)
        terms = sbuf("terms", [P, TOP, T], F32)
        sums_sb = sbuf("sums_sb", [P, T // P, N], F32)
        o_banks = [bank(number, "o_bank", [P, P]) for number in (4, 5, 6, 0)]
        halves = pieces((0, T // 2, T))
        for lo, hi in halves:
            blocks = range(lo // P, hi // P)
            nc.scalar.activation(raw[:, lo:hi], y_sb[:].indirect(entries(pos_sb[0], lo, hi)), COPY)
            nc.vector.tensor_tensor(terms[:, 1, lo:hi], y_sb[:].indirect(entries(pos_sb[1], lo, hi)), gate_sb[:, 1, lo:hi], MULT)
            add_turned(terms[:, 1, :], blocks, False)
            nc.vector.tensor_tensor(terms[:, 0, lo:hi], raw[:, lo:hi], gate_sb[:, 0, lo:hi], MULT)
            add_turned(terms[:, 0, :], blocks, True)
        for tile, group in zip(sums, groups):
            nc.scalar.copy(sums_sb[:, group[0] : group[-1] + 1, :], tile[:])
            for b in group:
                nc.tensor.transpose(o_banks[b][:], sums_sb[:, b, :], identity[:])
        for lo, hi in halves:
            nc.vector.tensor_tensor(terms[:, 2, lo:hi], y_sb[:].indirect(entries(pos_sb[2], lo, hi)), gate_sb[:, 2, lo:hi], MULT)

        result = sbuf("result", [P, T], F32)
        for b in range(T // P):
            tokens = slice(b * P, (b + 1) * P)
            nc.vector.tensor_tensor(result[:, tokens], o_banks[b][:], terms[:, 2, tokens], ADD)
            (nc.scalar, nc.sync)[b % 2].dma_start(out[:, tokens], result[:, tokens])
